import numpy as np
import ml_dtypes


def mxq(x, axis, fmt="e4m3"):
    dtype, down = {"e4m3": (ml_dtypes.float8_e4m3fn, 7), "e5m2": (ml_dtypes.float8_e5m2, 14)}[fmt]
    v = np.moveaxis(np.asarray(x, np.float32).astype(ml_dtypes.bfloat16).astype(np.float64), axis, -1)
    blocks = v.reshape(v.shape[:-1] + (-1, 32))
    amax = np.abs(blocks).max(-1, keepdims=True)
    byte = np.maximum(np.where(amax > 0, np.frexp(amax)[1] - 1 + 127, 0) - down, 1)
    scale = np.exp2(byte - 127.0)
    codes = (blocks / scale).astype(np.float32).astype(dtype).astype(np.float64)
    return np.moveaxis((codes * scale).reshape(v.shape), -1, axis)


WIDE = False


def mx_kscale(k):
    if not WIDE:
        return np.ones(k)
    levels = np.array([10, -10, 5, -5, 0])
    if k % 512:
        return np.exp2(np.random.permutation(np.resize(levels, k // 32))).repeat(32)
    a = np.empty((k // 512, 16))
    for p in range(k // 512):
        a[p, :8] = np.random.permutation(np.resize(levels, 8))
        for g in range(8):
            far = levels[np.abs(levels - a[p, g]) >= 10]
            a[p, g + 8] = far[np.random.randint(len(far))]
    return np.exp2(a.ravel()).repeat(32)


def f64(x):
    return np.asarray(x).astype(np.float64)


def striped(idx):
    return np.tile(idx.reshape(-1, 16).T, (8, 1)).astype(np.uint16)


def unstriped(offs):
    return offs[:16].T.reshape(-1).astype(np.int64)


E2M1 = np.array([0.0, 0.5, 1.0, 1.5, 2.0, 3.0, 4.0, 6.0, -0.0, -0.5, -1.0, -1.5, -2.0, -3.0, -4.0, -6.0])


def pack_weight(w, fmt):
    k, n = w.shape
    w = f64(np.asarray(w, np.float32).astype(ml_dtypes.bfloat16)).reshape(k // 32, 32, n)
    amax = np.abs(w).max(1)
    if fmt == "e4m3":
        byte = np.frexp(amax)[1] - 1 + 127 - 7
    else:
        mant, ex = np.frexp(amax / 6.0)
        byte = np.where(mant > 0.5, ex, ex - 1) + 127
    byte = np.clip(np.where(amax > 0, byte, 1), 1, 254)
    scaled = (w * np.exp2(127.0 - byte)[:, None, :]).reshape(k, n).astype(np.float32)
    by_word = np.ascontiguousarray(scaled.reshape(k // 512, 128, 4, n).transpose(0, 1, 3, 2))
    if fmt == "e4m3":
        words = by_word.astype(ml_dtypes.float8_e4m3fn).view(np.uint8)
    else:
        c = by_word.astype(ml_dtypes.float4_e2m1fn).view(np.uint8) & 0xF
        words = (c[..., 0::2] | (c[..., 1::2] << 4)).reshape(k // 512, 128, 2 * n)
    return np.ascontiguousarray(words), np.ascontiguousarray(byte.astype(np.uint8).reshape(k // 512, 16, n))


def unpack_weight(words, scales, fmt):
    g, _, n = scales.shape
    words = np.ascontiguousarray(words).reshape(g, 128, n, -1)
    if fmt == "e4m3":
        vals = words.view(ml_dtypes.float8_e4m3fn).astype(np.float64)
    else:
        nib = np.empty((g, 128, n, 4), np.uint8)
        nib[..., 0::2] = words & 0xF
        nib[..., 1::2] = words >> 4
        vals = E2M1[nib]
    vals = vals * np.repeat(np.exp2(scales.astype(np.float64) - 127.0), 8, axis=1)[..., None]
    return vals.transpose(0, 1, 3, 2).reshape(g * 512, n)


def gelu(v):
    return 0.5 * v * (1.0 + np.tanh(np.sqrt(2.0 / np.pi) * (v + 0.044715 * v**3)))


K, T, S, H, N, T2 = 1024, 2048, 1024, 512, 384, 2048

def setup_inputs():
    n = np.random.standard_normal
    s = mx_kscale(K)[:, None]
    u = mx_kscale(H)[:, None]
    tab_words, tab_scales = pack_weight(n((K, T)) * s, "e4m3")
    gl_words, gl_scales = pack_weight(n((K, H)) / s / np.sqrt(K), "e2m1")
    gr_words, gr_scales = pack_weight(n((K, H)) / s / np.sqrt(K), "e2m1")
    wo_words, wo_scales = pack_weight(n((H, N)) / u / np.sqrt(H), "e4m3")
    return {
        "tab_words": tab_words, "tab_scales": tab_scales,
        "offs": striped(np.random.permutation(T)[:S]),
        "wl": (1.5 * n((K, H)) / s * u.T / np.sqrt(K)).astype(np.float32),
        "wr": (1.5 * n((K, H)) / s / np.sqrt(K)).astype(np.float32),
        "gl_words": gl_words, "gl_scales": gl_scales,
        "gr_words": gr_words, "gr_scales": gr_scales,
        "wo_words": wo_words, "wo_scales": wo_scales,
        "wgo": np.exp(0.3 * n((128, S))).astype(np.float32),
        "offs2": striped(np.random.permutation(T2)[:S]),
    }

def reference(tab_words, tab_scales, offs, wl, wr, gl_words, gl_scales, gr_words, gr_scales, wo_words, wo_scales, wgo, offs2):
    v = unpack_weight(tab_words, tab_scales, "e4m3")[:, unstriped(offs)]
    left = mxq(f64(wl), 0, "e4m3").T @ v
    right = mxq(f64(wr), 0, "e4m3").T @ v
    gl = unpack_weight(gl_words, gl_scales, "e2m1").T @ v
    gr = unpack_weight(gr_words, gr_scales, "e2m1").T @ v
    h = (left * (1 / (1 + np.exp(-gl)))) * (right * (1 / (1 + np.exp(-gr))))
    y = unpack_weight(wo_words, wo_scales, "e4m3").T @ mxq(h, 0, "e4m3")
    out = np.zeros((N, T2))
    out[:, unstriped(offs2)] = np.tile(f64(wgo), (N // 128, 1)) * y
    return out

@@ -1,0 +1,220 @@
+from contextlib import ExitStack
+
+import concourse.mybir as mybir
+from concourse.masks import make_identity
+
+K, T, S, H, N, T2 = 1024, 2048, 1024, 512, 384, 2048
+FLOPS = 2 * (4 * K * H * S + H * N * S)
+
+F32 = mybir.dt.float32
+BF16 = mybir.dt.bfloat16
+I32 = mybir.dt.int32
+U32 = mybir.dt.uint32
+U16 = mybir.dt.uint16
+U8 = mybir.dt.uint8
+FP8X4 = mybir.dt.float8_e4m3fn_x4
+FP4X4 = mybir.dt.float4_e2m1fn_x4
+MULT = mybir.AluOpType.mult
+SIGMOID = mybir.ActivationFunctionType.Sigmoid
+
+P = 128
+PASSES = K // 512
+HALF = S // 2
+CHUNK = 256
+ROW_TILES = N // P
+
+
+def tile_list_gated_pair_terms_kernel(
+    tc, tab_words, tab_scales, offs, wl, wr, gl_words, gl_scales, gr_words, gr_scales,
+    wo_words, wo_scales, wgo, offs2, out,
+):
+    nc = tc.nc
+    with ExitStack() as ctx:
+        lists = ctx.enter_context(tc.tile_pool(name="lists", bufs=1))
+        keep = ctx.enter_context(tc.tile_pool(name="keep", bufs=1))
+        psum = ctx.enter_context(tc.psum_pool(name="psum", bufs=1))
+
+        def held(shape, dtype, name):
+            return keep.tile(shape, dtype, name=name, align_bytes=64)
+
+        pick = lists.tile([P, S // 16], U16, name="pick")
+        place = lists.tile([P, S // 16], U16, name="place")
+
+        tab_w = [held([P, T], I32, "tab_w%d" % a) for a in range(PASSES)]
+        tab_s = held([P, T], U8, "tab_s")
+        v_w = [[held([P, HALF], U32, "v_w%d%d" % (a, h)) for h in range(2)] for a in range(PASSES)]
+        v_s = [[held([P, HALF], U8, "v_s%d%d" % (a, h)) for h in range(2)] for a in range(PASSES)]
+        gate_w = [held([P, PASSES * 2 * H], U8, "gate_w%d" % g) for g in range(2)]
+        gate_s = [held([P, PASSES * H], U8, "gate_s%d" % g) for g in range(2)]
+        raw = [[held([P, 4, H], F32, "raw%d%d" % (g, a)) for a in range(PASSES)] for g in range(2)]
+        woven = [[held([P, H, 4], BF16, "woven%d%d" % (g, a)) for a in range(PASSES)] for g in range(2)]
+        proj_w = [[held([P, H], U32, "proj_w%d%d" % (g, a)) for a in range(PASSES)] for g in range(2)]
+        proj_s = [[held([P, H], U8, "proj_s%d%d" % (g, a)) for a in range(PASSES)] for g in range(2)]
+        wo_w = held([P, N], I32, "wo_w")
+        wo_s = held([P, N], U8, "wo_s")
+        wgo_sb = held([P, S], F32, "wgo_sb")
+        cache = [held([P, T2], F32, "cache%d" % n) for n in range(ROW_TILES)]
+        y_sb = held([P, ROW_TILES, S], F32, "y_sb")
+        ident = held([P, P], F32, "ident")
+
+        nc.vector.memset(tab_s[:].bitcast(I32), 0)
+        nc.vector.memset(gate_s[1][:].bitcast(I32), 0)
+        nc.gpsimd.memset(gate_s[0][:].bitcast(I32), 0)
+        nc.vector.memset(wo_s[:].bitcast(I32), 0)
+        for h in range(2):
+            nc.vector.memset(v_s[1][h][:].bitcast(I32), 0)
+
+        def load_raw(g, a):
+            w = (wl, wr)[g]
+            nc.sync.dma_start(out=raw[g][a][:], in_=w[512 * a : 512 * (a + 1), :].rearrange("(p j) c -> p j c", j=4))
+
+        def load_table(a):
+            nc.sync.dma_start(out=tab_w[a][:], in_=tab_words[a].rearrange("p t i -> p (t i)").bitcast(I32))
+
+        def load_gate_words(g):
+            nc.sync.dma_start(
+                out=gate_w[g][:].bitcast(I32).rearrange("p (a c) -> p a c", a=PASSES),
+                in_=(gl_words, gr_words)[g].bitcast(I32).rearrange("a p c -> p a c"),
+            )
+
+        def load_gate_scales(queue, g, q):
+            queue.dma_start(
+                out=gate_s[g][:].bitcast(I32).rearrange("p (a c) -> p a c", a=PASSES)[32 * q : 32 * q + 4],
+                in_=(gl_scales, gr_scales)[g].bitcast(I32)[:, 4 * q : 4 * q + 4, :].rearrange("a r c -> r a c"),
+            )
+
+        nc.sync.dma_start(pick[:], offs)
+        load_table(0)
+        for q in range(4):
+            nc.sync.dma_start(
+                out=tab_s[:].bitcast(I32)[32 * q : 32 * q + 8, :],
+                in_=tab_scales.bitcast(I32)[:, 4 * q : 4 * q + 4, :],
+            )
+        load_table(1)
+        load_raw(0, 0)
+        for q in range(4):
+            load_gate_scales(nc.sync, 1, q)
+        load_gate_words(0)
+        load_gate_words(1)
+        load_raw(0, 1)
+        load_raw(1, 0)
+        load_raw(1, 1)
+        nc.sync.dma_start(out=wo_w[:], in_=wo_words[0].rearrange("p c i -> p (c i)").bitcast(I32))
+        for q in range(4):
+            nc.sync.dma_start(
+                out=wo_s[:].bitcast(I32)[32 * q : 32 * q + 4, :],
+                in_=wo_scales[0].bitcast(I32)[4 * q : 4 * q + 4, :],
+            )
+        nc.sync.dma_start(place[:], offs2)
+        nc.sync.dma_start(out=wgo_sb[:], in_=wgo)
+
+        for q in range(4):
+            load_gate_scales(nc.gpsimd, 0, q)
+        make_identity(nc, ident[:])
+
+        for n in range(ROW_TILES):
+            nc.vector.memset(cache[n][:], 0.0)
+
+        for h in range(2):
+            entries = pick[:, h * (HALF // 16) : (h + 1) * (HALF // 16)]
+            nc.vector.tensor_copy(v_s[0][h][:], tab_s[:].indirect(entries))
+            nc.gpsimd.dma_start(out=v_s[1][h][:].bitcast(I32)[0 : P - 4, :], in_=v_s[0][h][:].bitcast(I32)[4:P, :])
+            for a in range(PASSES):
+                nc.vector.tensor_copy(v_w[a][h][:], tab_w[a][:].bitcast(U32).indirect(entries))
+
+        for g in range(2):
+            for a in range(PASSES):
+                dst = woven[g][a][:].rearrange("p (c i) j -> p c j i", i=4)
+                src = raw[g][a][:].rearrange("p j (c i) -> p c j i", i=4)
+                if a == 0:
+                    nc.scalar.copy(dst, src)
+                else:
+                    nc.vector.tensor_copy(dst, src)
+                nc.vector.quantize_mx(
+                    out=proj_w[g][a][:].bitcast(FP8X4),
+                    scales=proj_s[g][a][:],
+                    in_=woven[g][a][:].rearrange("p c j -> p (c j)"),
+                )
+
+        def project(bank, i, words, scales):
+            h, j = divmod(i * P, HALF)
+            for a in range(PASSES):
+                nc.tensor.matmul_mx(
+                    out=bank[:],
+                    lhsT=v_w[a][h][:, j : j + P].bitcast(FP8X4),
+                    lhsT_scale=v_s[a][h][:, j : j + P],
+                    rhs=words(a),
+                    rhs_scale=scales(a),
+                    start=(a == 0),
+                    stop=(a == PASSES - 1),
+                )
+
+        def from_bank(bank):
+            return bank[:].rearrange("t (p u e) -> t u p e", u=2, e=2)
+
+        def in_order(tile):
+            return tile[:].rearrange("t (u p e) -> t u p e", u=2, e=2)
+
+        both = []
+        for i in range(S // P):
+            sig = []
+            for g in range(2):
+                bank = psum.tile([P, H], F32, name="gate_bank", bufs=2)
+                project(
+                    bank, i,
+                    lambda a: gate_w[g][:, 2 * H * a : 2 * H * (a + 1)].bitcast(FP4X4),
+                    lambda a: gate_s[g][:, H * a : H * (a + 1)],
+                )
+                one = keep.tile([P, H], F32, name="sig%d" % g, bufs=3)
+                nc.scalar.activation(in_order(one), from_bank(bank), SIGMOID)
+                sig.append(one)
+            product = keep.tile([P, H], F32, name="both", bufs=S // P)
+            nc.vector.tensor_tensor(product[:], sig[0][:], sig[1][:], MULT)
+            both.append(product)
+
+        for c in range(S // CHUNK):
+            turned = psum.tile([P, 4, P], F32, name="turned")
+            for ii in range(CHUNK // P):
+                i = c * (CHUNK // P) + ii
+                left = psum.tile([P, H], F32, name="left", tag="proj", bufs=3)
+                project(left, i, lambda a: proj_w[0][a][:].bitcast(FP8X4), lambda a: proj_s[0][a][:])
+                gated = keep.tile([P, H], F32, name="gated", bufs=S // P)
+                nc.vector.tensor_tensor(in_order(gated), from_bank(left), in_order(both[i]), MULT)
+                right = psum.tile([P, H], F32, name="right", tag="proj", bufs=3)
+                project(right, i, lambda a: proj_w[1][a][:].bitcast(FP8X4), lambda a: proj_s[1][a][:])
+                h_rows = keep.tile([P, H], BF16, name="h_rows", bufs=4)
+                nc.vector.tensor_tensor(in_order(h_rows), from_bank(right), in_order(gated), MULT)
+                for u in range(2):
+                    nc.tensor.transpose(turned[:, 2 * ii + u, :], h_rows[:].bitcast(F32)[:, P * u : P * (u + 1)], ident[:])
+            h_cols = keep.tile([P, CHUNK * 4], BF16, name="h_cols", bufs=2, align_bytes=64)
+            nc.scalar.copy(
+                h_cols[:].bitcast(F32).rearrange("p (i t u) -> p i t u", i=CHUNK // P, u=2),
+                turned[:].rearrange("p (i u) t -> p i t u", u=2),
+            )
+            h_w = keep.tile([P, CHUNK], U32, name="h_w", bufs=2, align_bytes=64)
+            h_s = keep.tile([P, CHUNK], U8, name="h_s", bufs=2, align_bytes=64)
+            nc.vector.quantize_mx(out=h_w[:].bitcast(FP8X4), scales=h_s[:], in_=h_cols[:])
+            y_two = psum.tile([P, 2, CHUNK], F32, name="y_two")
+            y_one = psum.tile([P, CHUNK], F32, name="y_one")
+            for n in range(ROW_TILES):
+                nc.tensor.matmul_mx(
+                    out=y_two[:, n, :] if n < 2 else y_one[:],
+                    lhsT=wo_w[:, n * P : (n + 1) * P].bitcast(FP8X4),
+                    lhsT_scale=wo_s[:, n * P : (n + 1) * P],
+                    rhs=h_w[:].bitcast(FP8X4),
+                    rhs_scale=h_s[:],
+                    start=True,
+                    stop=True,
+                )
+            cols = slice(c * CHUNK, (c + 1) * CHUNK)
+            nc.scalar.copy(y_sb[:, 0:2, cols], y_two[:])
+            nc.scalar.copy(y_sb[:, 2, cols], y_one[:])
+
+        for lo, hi in ((0, 256), (256, 512), (512, 1024)):
+            for n in range(ROW_TILES):
+                nc.vector.tensor_tensor(
+                    cache[n][:].indirect(place[:, lo // 16 : hi // 16]),
+                    y_sb[:, n, lo:hi], wgo_sb[:, lo:hi], MULT,
+                )
+        for n in range(ROW_TILES):
+            nc.sync.dma_start(out=out[n * P : (n + 1) * P, :], in_=cache[n][:])

@@ -47,22 +47,15 @@ def tile_list_gated_pair_terms_kernel(
         gate_w = [held([P, PASSES * 2 * H], U8, "gate_w%d" % g) for g in range(2)]
         gate_s = [held([P, PASSES * H], U8, "gate_s%d" % g) for g in range(2)]
         raw = [[held([P, 4, H], F32, "raw%d%d" % (g, a)) for a in range(PASSES)] for g in range(2)]
-        woven = [[held([P, H, 4], BF16, "woven%d%d" % (g, a)) for a in range(PASSES)] for g in range(2)]
         proj_w = [[held([P, H], U32, "proj_w%d%d" % (g, a)) for a in range(PASSES)] for g in range(2)]
         proj_s = [[held([P, H], U8, "proj_s%d%d" % (g, a)) for a in range(PASSES)] for g in range(2)]
         wo_w = held([P, N], I32, "wo_w")
         wo_s = held([P, N], U8, "wo_s")
         wgo_sb = held([P, S], F32, "wgo_sb")
         cache = [held([P, T2], F32, "cache%d" % n) for n in range(ROW_TILES)]
-        y_sb = held([P, ROW_TILES, S], F32, "y_sb")
         ident = held([P, P], F32, "ident")
 
-        nc.vector.memset(tab_s[:].bitcast(I32), 0)
-        nc.vector.memset(gate_s[1][:].bitcast(I32), 0)
-        nc.gpsimd.memset(gate_s[0][:].bitcast(I32), 0)
-        nc.vector.memset(wo_s[:].bitcast(I32), 0)
-        for h in range(2):
-            nc.vector.memset(v_s[1][h][:].bitcast(I32), 0)
+        nc.gpsimd.memset(tab_s[:].bitcast(I32), 0)
 
         def load_raw(g, a):
             w = (wl, wr)[g]
@@ -92,11 +85,13 @@ def tile_list_gated_pair_terms_kernel(
             )
         load_table(1)
         load_raw(0, 0)
-        for q in range(4):
-            load_gate_scales(nc.sync, 1, q)
         load_gate_words(0)
         load_gate_words(1)
+        for q in range(4):
+            load_gate_scales(nc.sync, 0, q)
         load_raw(0, 1)
+        for q in range(4):
+            load_gate_scales(nc.sync, 1, q)
         load_raw(1, 0)
         load_raw(1, 1)
         nc.sync.dma_start(out=wo_w[:], in_=wo_words[0].rearrange("p c i -> p (c i)").bitcast(I32))
@@ -108,33 +103,31 @@ def tile_list_gated_pair_terms_kernel(
         nc.sync.dma_start(place[:], offs2)
         nc.sync.dma_start(out=wgo_sb[:], in_=wgo)
 
-        for q in range(4):
-            load_gate_scales(nc.gpsimd, 0, q)
+        nc.vector.memset(cache[0][:], 0.0)
+        nc.gpsimd.memset(cache[1][:], 0.0)
+        nc.gpsimd.memset(cache[2][:], 0.0)
         make_identity(nc, ident[:])
-
-        for n in range(ROW_TILES):
-            nc.vector.memset(cache[n][:], 0.0)
 
         for h in range(2):
             entries = pick[:, h * (HALF // 16) : (h + 1) * (HALF // 16)]
+            nc.vector.tensor_copy(v_w[0][h][:], tab_w[0][:].bitcast(U32).indirect(entries))
             nc.vector.tensor_copy(v_s[0][h][:], tab_s[:].indirect(entries))
             nc.gpsimd.dma_start(out=v_s[1][h][:].bitcast(I32)[0 : P - 4, :], in_=v_s[0][h][:].bitcast(I32)[4:P, :])
-            for a in range(PASSES):
-                nc.vector.tensor_copy(v_w[a][h][:], tab_w[a][:].bitcast(U32).indirect(entries))
+            nc.vector.tensor_copy(v_w[1][h][:], tab_w[1][:].bitcast(U32).indirect(entries))
 
-        for g in range(2):
-            for a in range(PASSES):
-                dst = woven[g][a][:].rearrange("p (c i) j -> p c j i", i=4)
-                src = raw[g][a][:].rearrange("p j (c i) -> p c j i", i=4)
-                if a == 0:
-                    nc.scalar.copy(dst, src)
-                else:
-                    nc.vector.tensor_copy(dst, src)
-                nc.vector.quantize_mx(
-                    out=proj_w[g][a][:].bitcast(FP8X4),
-                    scales=proj_s[g][a][:],
-                    in_=woven[g][a][:].rearrange("p c j -> p (c j)"),
-                )
+        def quantise_weight(g, a, tag):
+            woven = keep.tile([P, H, 4], BF16, name="woven", tag=tag, align_bytes=64)
+            dst = woven[:].rearrange("p (c i) j -> p c j i", i=4)
+            src = raw[g][a][:].rearrange("p j (c i) -> p c j i", i=4)
+            if a == 0:
+                nc.scalar.copy(dst, src)
+            else:
+                nc.vector.tensor_copy(dst, src)
+            nc.vector.quantize_mx(
+                out=proj_w[g][a][:].bitcast(FP8X4),
+                scales=proj_s[g][a][:],
+                in_=woven[:].rearrange("p c j -> p (c j)"),
+            )
 
         def project(bank, i, words, scales):
             h, j = divmod(i * P, HALF)
@@ -153,68 +146,105 @@ def tile_list_gated_pair_terms_kernel(
             return bank[:].rearrange("t (p u e) -> t u p e", u=2, e=2)
 
         def in_order(tile):
-            return tile[:].rearrange("t (u p e) -> t u p e", u=2, e=2)
+            return tile.rearrange("t (u p e) -> t u p e", u=2, e=2)
 
-        both = []
-        for i in range(S // P):
-            sig = []
-            for g in range(2):
-                bank = psum.tile([P, H], F32, name="gate_bank", bufs=2)
+        h_cols = [held([P, HALF * 4], BF16, "h_cols%d" % h) for h in range(2)]
+        h_w = [held([P, HALF], U32, "h_w%d" % h) for h in range(2)]
+        h_s = [held([P, HALF], U8, "h_s%d" % h) for h in range(2)]
+
+        def out_project(h, n, y):
+            bank = psum.tile([P, HALF], F32, name="y_bank", tag="wide", bufs=3)
+            nc.tensor.matmul_mx(
+                out=bank[:],
+                lhsT=wo_w[:, n * P : (n + 1) * P].bitcast(FP8X4),
+                lhsT_scale=wo_s[:, n * P : (n + 1) * P],
+                rhs=h_w[h][:].bitcast(FP8X4),
+                rhs_scale=h_s[h][:],
+                start=True,
+                stop=True,
+            )
+            nc.scalar.copy(y, bank[:])
+            return y
+
+        def scatter(h, n, y):
+            nc.vector.tensor_tensor(
+                cache[n][:].indirect(place[:, h * (HALF // 16) : (h + 1) * (HALF // 16)]),
+                y, wgo_sb[:, h * HALF : (h + 1) * HALF], MULT,
+            )
+
+        def pair(name, tag):
+            return keep.tile([P, 2, H], F32, name=name, tag=tag, align_bytes=64)[:]
+
+        def gate(g, c, sig):
+            for ii in range(2):
+                bank = psum.tile([P, H], F32, name="gate_bank", tag="wide", bufs=3)
                 project(
-                    bank, i,
+                    bank, 2 * c + ii,
                     lambda a: gate_w[g][:, 2 * H * a : 2 * H * (a + 1)].bitcast(FP4X4),
                     lambda a: gate_s[g][:, H * a : H * (a + 1)],
                 )
-                one = keep.tile([P, H], F32, name="sig%d" % g, bufs=3)
-                nc.scalar.activation(in_order(one), from_bank(bank), SIGMOID)
-                sig.append(one)
-            product = keep.tile([P, H], F32, name="both", bufs=S // P)
-            nc.vector.tensor_tensor(product[:], sig[0][:], sig[1][:], MULT)
-            both.append(product)
+                nc.scalar.activation(in_order(sig[:, ii, :]), from_bank(bank), SIGMOID)
+            return sig
 
-        for c in range(S // CHUNK):
-            turned = psum.tile([P, 4, P], F32, name="turned")
-            for ii in range(CHUNK // P):
-                i = c * (CHUNK // P) + ii
+        def gated_left(c, sig):
+            once = pair("once", "once%d" % c)
+            for ii in range(2):
                 left = psum.tile([P, H], F32, name="left", tag="proj", bufs=3)
-                project(left, i, lambda a: proj_w[0][a][:].bitcast(FP8X4), lambda a: proj_s[0][a][:])
-                gated = keep.tile([P, H], F32, name="gated", bufs=S // P)
-                nc.vector.tensor_tensor(in_order(gated), from_bank(left), in_order(both[i]), MULT)
+                project(left, 2 * c + ii, lambda a: proj_w[0][a][:].bitcast(FP8X4), lambda a: proj_s[0][a][:])
+                nc.vector.tensor_tensor(in_order(once[:, ii, :]), from_bank(left), in_order(sig[:, ii, :]), MULT)
+            return once
+
+        def gated_twice(c, once, sig, tag):
+            twice = pair("twice", tag)
+            nc.vector.tensor_tensor(twice, once, sig, MULT)
+            return twice
+
+        def times_right(c, gated):
+            turned = psum.tile([P, 4, P], F32, name="turned", bufs=2)
+            for ii in range(2):
                 right = psum.tile([P, H], F32, name="right", tag="proj", bufs=3)
-                project(right, i, lambda a: proj_w[1][a][:].bitcast(FP8X4), lambda a: proj_s[1][a][:])
-                h_rows = keep.tile([P, H], BF16, name="h_rows", bufs=4)
-                nc.vector.tensor_tensor(in_order(h_rows), from_bank(right), in_order(gated), MULT)
+                project(right, 2 * c + ii, lambda a: proj_w[1][a][:].bitcast(FP8X4), lambda a: proj_s[1][a][:])
+                h_rows = keep.tile([P, H], BF16, name="h_rows", tag="h_rows%d" % (2 * c + ii))
+                nc.vector.tensor_tensor(in_order(h_rows[:]), from_bank(right), in_order(gated[:, ii, :]), MULT)
                 for u in range(2):
                     nc.tensor.transpose(turned[:, 2 * ii + u, :], h_rows[:].bitcast(F32)[:, P * u : P * (u + 1)], ident[:])
-            h_cols = keep.tile([P, CHUNK * 4], BF16, name="h_cols", bufs=2, align_bytes=64)
+            h, cc = divmod(c, 2)
             nc.scalar.copy(
-                h_cols[:].bitcast(F32).rearrange("p (i t u) -> p i t u", i=CHUNK // P, u=2),
+                h_cols[h][:].bitcast(F32)[:, cc * 2 * CHUNK : (cc + 1) * 2 * CHUNK].rearrange("p (i t u) -> p i t u", i=2, u=2),
                 turned[:].rearrange("p (i u) t -> p i t u", u=2),
             )
-            h_w = keep.tile([P, CHUNK], U32, name="h_w", bufs=2, align_bytes=64)
-            h_s = keep.tile([P, CHUNK], U8, name="h_s", bufs=2, align_bytes=64)
-            nc.vector.quantize_mx(out=h_w[:].bitcast(FP8X4), scales=h_s[:], in_=h_cols[:])
-            y_two = psum.tile([P, 2, CHUNK], F32, name="y_two")
-            y_one = psum.tile([P, CHUNK], F32, name="y_one")
-            for n in range(ROW_TILES):
-                nc.tensor.matmul_mx(
-                    out=y_two[:, n, :] if n < 2 else y_one[:],
-                    lhsT=wo_w[:, n * P : (n + 1) * P].bitcast(FP8X4),
-                    lhsT_scale=wo_s[:, n * P : (n + 1) * P],
-                    rhs=h_w[:].bitcast(FP8X4),
-                    rhs_scale=h_s[:],
-                    start=True,
-                    stop=True,
-                )
-            cols = slice(c * CHUNK, (c + 1) * CHUNK)
-            nc.scalar.copy(y_sb[:, 0:2, cols], y_two[:])
-            nc.scalar.copy(y_sb[:, 2, cols], y_one[:])
+            if cc == 1:
+                nc.vector.quantize_mx(out=h_w[h][:].bitcast(FP8X4), scales=h_s[h][:], in_=h_cols[h][:])
 
-        for lo, hi in ((0, 256), (256, 512), (512, 1024)):
-            for n in range(ROW_TILES):
-                nc.vector.tensor_tensor(
-                    cache[n][:].indirect(place[:, lo // 16 : hi // 16]),
-                    y_sb[:, n, lo:hi], wgo_sb[:, lo:hi], MULT,
-                )
+        quantise_weight(0, 0, "woven00")
+        quantise_weight(0, 1, "woven01")
+        sig_l0 = gate(0, 0, pair("sig_l0", "sig_l0"))
+        sig_l1 = gate(0, 1, pair("sig_l1", "sig_l1"))
+        once0 = gated_left(0, sig_l0)
+        once1 = gated_left(1, sig_l1)
+        twice0 = gated_twice(0, once0, gate(1, 0, pair("sig_r0", "sig_r0")), "twice0")
+        sig_r1 = gate(1, 1, pair("sig_r1", "sig_r1"))
+        quantise_weight(1, 0, "woven10")
+        quantise_weight(1, 1, "sig_r0")
+        twice1 = gated_twice(1, once1, sig_r1, "twice1")
+        times_right(0, twice0)
+        times_right(1, twice1)
+        late = keep.tile([P, 2, 2, H], F32, name="late", tag="raw10", align_bytes=64)
+        once2 = gated_left(2, gate(0, 2, late[:, 0]))
+        twice2 = gated_twice(2, once2, gate(1, 2, late[:, 1]), "twice2")
+        y_first = keep.tile([P, HALF], F32, name="y_first", tag="twice3", align_bytes=64)
+        out_project(0, 0, y_first[:])
+        times_right(2, twice2)
+        once3 = gated_left(3, gate(0, 3, pair("sig_l3", "sig_l0")))
+        sig_r3 = gate(1, 3, pair("sig_r3", "sig_l1"))
+        scatter(0, 0, y_first[:])
+        times_right(3, gated_twice(3, once3, sig_r3, "twice3"))
+        y_rest = keep.tile([P, 2, HALF], F32, name="y_rest", tag="h_rows7")
+        for n in range(1, ROW_TILES):
+            scatter(0, n, out_project(0, n, y_rest[:, n - 1, :]))
+        y_last = held([P, ROW_TILES, HALF], F32, "y_last")
         for n in range(ROW_TILES):
-            nc.sync.dma_start(out=out[n * P : (n + 1) * P, :], in_=cache[n][:])
+            scatter(1, n, out_project(1, n, y_last[:, n, :]))
+        for n in range(ROW_TILES):
+            for queue, cols in ((nc.sync, slice(0, T2 // 2)), (nc.scalar, slice(T2 // 2, T2))):
+                queue.dma_start(out=out[n * P : (n + 1) * P, cols], in_=cache[n][:, cols])

@@ -41,8 +41,7 @@ def tile_list_gated_pair_terms_kernel(
         place = lists.tile([P, S // 16], U16, name="place")
 
         tab_w = [held([P, T], I32, "tab_w%d" % a) for a in range(PASSES)]
-        tab_s = held([P, T], U8, "tab_s")
-        v_w = [[held([P, HALF], U32, "v_w%d%d" % (a, h)) for h in range(2)] for a in range(PASSES)]
+        tab_s = held([P, PASSES * T], U8, "tab_s")
         v_s = [[held([P, HALF], U8, "v_s%d%d" % (a, h)) for h in range(2)] for a in range(PASSES)]
         gate_w = [held([P, PASSES * 2 * H], U8, "gate_w%d" % g) for g in range(2)]
         gate_s = [held([P, PASSES * H], U8, "gate_s%d" % g) for g in range(2)]
@@ -55,7 +54,8 @@ def tile_list_gated_pair_terms_kernel(
         cache = [held([P, T2], F32, "cache%d" % n) for n in range(ROW_TILES)]
         ident = held([P, P], F32, "ident")
 
-        nc.gpsimd.memset(tab_s[:].bitcast(I32), 0)
+        nc.vector.memset(tab_s[:, 0:T].bitcast(I32), 0)
+        nc.gpsimd.memset(tab_s[:, T : 2 * T].bitcast(I32), 0)
 
         def load_raw(g, a):
             w = (wl, wr)[g]
@@ -72,7 +72,7 @@ def tile_list_gated_pair_terms_kernel(
 
         def load_gate_scales(queue, g, q):
             queue.dma_start(
-                out=gate_s[g][:].bitcast(I32).rearrange("p (a c) -> p a c", a=PASSES)[32 * q : 32 * q + 4],
+                out=gate_s[g][:].bitcast(I32)[32 * q : 32 * q + 4, :],
                 in_=(gl_scales, gr_scales)[g].bitcast(I32)[:, 4 * q : 4 * q + 4, :].rearrange("a r c -> r a c"),
             )
 
@@ -80,19 +80,19 @@ def tile_list_gated_pair_terms_kernel(
         load_table(0)
         for q in range(4):
             nc.sync.dma_start(
-                out=tab_s[:].bitcast(I32)[32 * q : 32 * q + 8, :],
-                in_=tab_scales.bitcast(I32)[:, 4 * q : 4 * q + 4, :],
+                out=tab_s[:].bitcast(I32)[32 * q : 32 * q + 4, :],
+                in_=tab_scales.bitcast(I32)[:, 4 * q : 4 * q + 4, :].rearrange("a r t -> r a t"),
             )
         load_table(1)
         load_raw(0, 0)
+        load_raw(0, 1)
         load_gate_words(0)
         load_gate_words(1)
         for q in range(4):
             load_gate_scales(nc.sync, 0, q)
-        load_raw(0, 1)
+        load_raw(1, 0)
         for q in range(4):
             load_gate_scales(nc.sync, 1, q)
-        load_raw(1, 0)
         load_raw(1, 1)
         nc.sync.dma_start(out=wo_w[:], in_=wo_words[0].rearrange("p c i -> p (c i)").bitcast(I32))
         for q in range(4):
@@ -103,23 +103,28 @@ def tile_list_gated_pair_terms_kernel(
         nc.sync.dma_start(place[:], offs2)
         nc.sync.dma_start(out=wgo_sb[:], in_=wgo)
 
-        nc.vector.memset(cache[0][:], 0.0)
-        nc.gpsimd.memset(cache[1][:], 0.0)
-        nc.gpsimd.memset(cache[2][:], 0.0)
+        for n in range(ROW_TILES):
+            nc.vector.memset(cache[n][:].bitcast(I32), 0)
         make_identity(nc, ident[:])
 
-        for h in range(2):
-            entries = pick[:, h * (HALF // 16) : (h + 1) * (HALF // 16)]
-            nc.vector.tensor_copy(v_w[0][h][:], tab_w[0][:].bitcast(U32).indirect(entries))
-            nc.vector.tensor_copy(v_s[0][h][:], tab_s[:].indirect(entries))
-            nc.gpsimd.dma_start(out=v_s[1][h][:].bitcast(I32)[0 : P - 4, :], in_=v_s[0][h][:].bitcast(I32)[4:P, :])
-            nc.vector.tensor_copy(v_w[1][h][:], tab_w[1][:].bitcast(U32).indirect(entries))
+        def entries(h):
+            return pick[:, h * (HALF // 16) : (h + 1) * (HALF // 16)]
+
+        def gather_words(h, tag):
+            words = keep.tile([P, PASSES, HALF], U32, name="v_w", tag=tag, align_bytes=64)
+            for a in range(PASSES):
+                nc.vector.tensor_copy(words[:, a, :], tab_w[a][:].bitcast(U32).indirect(entries(h)))
+            return words
+
+        def gather_scales(h):
+            for a in range(PASSES):
+                nc.vector.tensor_copy(v_s[a][h][:], tab_s[:, a * T : (a + 1) * T].indirect(entries(h)))
 
         def quantise_weight(g, a, tag):
             woven = keep.tile([P, H, 4], BF16, name="woven", tag=tag, align_bytes=64)
             dst = woven[:].rearrange("p (c i) j -> p c j i", i=4)
             src = raw[g][a][:].rearrange("p j (c i) -> p c j i", i=4)
-            if a == 0:
+            if (g, a) != (1, 1):
                 nc.scalar.copy(dst, src)
             else:
                 nc.vector.tensor_copy(dst, src)
@@ -134,7 +139,7 @@ def tile_list_gated_pair_terms_kernel(
             for a in range(PASSES):
                 nc.tensor.matmul_mx(
                     out=bank[:],
-                    lhsT=v_w[a][h][:, j : j + P].bitcast(FP8X4),
+                    lhsT=v_w[h][:, a, j : j + P].bitcast(FP8X4),
                     lhsT_scale=v_s[a][h][:, j : j + P],
                     rhs=words(a),
                     rhs_scale=scales(a),
@@ -216,7 +221,11 @@ def tile_list_gated_pair_terms_kernel(
             if cc == 1:
                 nc.vector.quantize_mx(out=h_w[h][:].bitcast(FP8X4), scales=h_s[h][:], in_=h_cols[h][:])
 
+        v_w = [gather_words(0, "v_w0")]
+        gather_scales(0)
+        gather_scales(1)
         quantise_weight(0, 0, "woven00")
+        v_w.append(gather_words(1, "woven00"))
         quantise_weight(0, 1, "woven01")
         sig_l0 = gate(0, 0, pair("sig_l0", "sig_l0"))
         sig_l1 = gate(0, 1, pair("sig_l1", "sig_l1"))
@@ -239,9 +248,10 @@ def tile_list_gated_pair_terms_kernel(
         sig_r3 = gate(1, 3, pair("sig_r3", "sig_l1"))
         scatter(0, 0, y_first[:])
         times_right(3, gated_twice(3, once3, sig_r3, "twice3"))
-        y_rest = keep.tile([P, 2, HALF], F32, name="y_rest", tag="h_rows7")
-        for n in range(1, ROW_TILES):
-            scatter(0, n, out_project(0, n, y_rest[:, n - 1, :]))
+        y_second = keep.tile([P, HALF], F32, name="y_second", tag="once3", align_bytes=64)
+        scatter(0, 1, out_project(0, 1, y_second[:]))
+        y_third = keep.tile([P, HALF], F32, name="y_third", tag="h_rows7")
+        scatter(0, 2, out_project(0, 2, y_third[:]))
         y_last = held([P, ROW_TILES, HALF], F32, "y_last")
         for n in range(ROW_TILES):
             scatter(1, n, out_project(1, n, y_last[:, n, :]))

@@ -110,11 +110,8 @@ def tile_list_gated_pair_terms_kernel(
         def entries(h):
             return pick[:, h * (HALF // 16) : (h + 1) * (HALF // 16)]
 
-        def gather_words(h, tag):
-            words = keep.tile([P, PASSES, HALF], U32, name="v_w", tag=tag, align_bytes=64)
-            for a in range(PASSES):
-                nc.vector.tensor_copy(words[:, a, :], tab_w[a][:].bitcast(U32).indirect(entries(h)))
-            return words
+        def gather_words(words, h, a):
+            nc.vector.tensor_copy(words[:, a, :], tab_w[a][:].bitcast(U32).indirect(entries(h)))
 
         def gather_scales(h):
             for a in range(PASSES):
@@ -221,11 +218,15 @@ def tile_list_gated_pair_terms_kernel(
             if cc == 1:
                 nc.vector.quantize_mx(out=h_w[h][:].bitcast(FP8X4), scales=h_s[h][:], in_=h_cols[h][:])
 
-        v_w = [gather_words(0, "v_w0")]
+        v_w = [held([P, PASSES, HALF], U32, "v_w0")]
+        gather_words(v_w[0], 0, 0)
         gather_scales(0)
+        gather_words(v_w[0], 0, 1)
         gather_scales(1)
         quantise_weight(0, 0, "woven00")
-        v_w.append(gather_words(1, "woven00"))
+        v_w.append(keep.tile([P, PASSES, HALF], U32, name="v_w1", tag="woven00", align_bytes=64))
+        for a in range(PASSES):
+            gather_words(v_w[1], 1, a)
         quantise_weight(0, 1, "woven01")
         sig_l0 = gate(0, 0, pair("sig_l0", "sig_l0"))
         sig_l1 = gate(0, 1, pair("sig_l1", "sig_l1"))

@@ -32,34 +32,36 @@ def tile_list_gated_pair_terms_kernel(
     with ExitStack() as ctx:
         lists = ctx.enter_context(tc.tile_pool(name="lists", bufs=1))
         keep = ctx.enter_context(tc.tile_pool(name="keep", bufs=1))
+        shared = ctx.enter_context(tc.tile_pool(name="shared", bufs=1))
         psum = ctx.enter_context(tc.psum_pool(name="psum", bufs=1))
 
-        def held(shape, dtype, name):
-            return keep.tile(shape, dtype, name=name, align_bytes=64)
+        def held(shape, dtype, name, tag=None):
+            return keep.tile(shape, dtype, name=name, tag=tag or name, align_bytes=64)
 
         pick = lists.tile([P, S // 16], U16, name="pick")
         place = lists.tile([P, S // 16], U16, name="place")
 
         tab_w = [held([P, T], I32, "tab_w%d" % a) for a in range(PASSES)]
-        tab_s = held([P, PASSES * T], U8, "tab_s")
-        v_s = [[held([P, HALF], U8, "v_s%d%d" % (a, h)) for h in range(2)] for a in range(PASSES)]
-        gate_w = [held([P, PASSES * 2 * H], U8, "gate_w%d" % g) for g in range(2)]
-        gate_s = [held([P, PASSES * H], U8, "gate_s%d" % g) for g in range(2)]
-        raw = [[held([P, 4, H], F32, "raw%d%d" % (g, a)) for a in range(PASSES)] for g in range(2)]
+        tab_s = shared.tile([P, T], U8, name="tab_s", align_bytes=64, offset=2048)
+        v_w = [[held([P, HALF], U32, "v_w%d%d" % (h, a)) for a in range(PASSES)] for h in range(2)]
+        v_s = [held([P, S], U8, "v_s%d" % a) for a in range(PASSES)]
+        gate_w = [held([P, PASSES * 2 * H], U8, "gate_w0")]
+        gate_s = [held([P, PASSES * H], U8, "gate_s0")]
+        raw = {}
         proj_w = [[held([P, H], U32, "proj_w%d%d" % (g, a)) for a in range(PASSES)] for g in range(2)]
         proj_s = [[held([P, H], U8, "proj_s%d%d" % (g, a)) for a in range(PASSES)] for g in range(2)]
-        wo_w = held([P, N], I32, "wo_w")
-        wo_s = held([P, N], U8, "wo_s")
-        wgo_sb = held([P, S], F32, "wgo_sb")
         cache = [held([P, T2], F32, "cache%d" % n) for n in range(ROW_TILES)]
         ident = held([P, P], F32, "ident")
 
-        nc.vector.memset(tab_s[:, 0:T].bitcast(I32), 0)
-        nc.gpsimd.memset(tab_s[:, T : 2 * T].bitcast(I32), 0)
+        nc.gpsimd.memset(tab_s[:].bitcast(I32), 0)
 
-        def load_raw(g, a):
+        def load_raw(g, a, tag):
             w = (wl, wr)[g]
-            nc.sync.dma_start(out=raw[g][a][:], in_=w[512 * a : 512 * (a + 1), :].rearrange("(p j) c -> p j c", j=4))
+            if g == a:
+                raw[g, a] = shared.tile([P, 4, H], F32, name="raw%d%d" % (g, a), align_bytes=64, offset=3136)
+            else:
+                raw[g, a] = held([P, 4, H], F32, "raw%d%d" % (g, a), tag)
+            nc.sync.dma_start(out=raw[g, a][:], in_=w[512 * a : 512 * (a + 1), :].rearrange("(p j) c -> p j c", j=4))
 
         def load_table(a):
             nc.sync.dma_start(out=tab_w[a][:], in_=tab_words[a].rearrange("p t i -> p (t i)").bitcast(I32))
@@ -70,61 +72,56 @@ def tile_list_gated_pair_terms_kernel(
                 in_=(gl_words, gr_words)[g].bitcast(I32).rearrange("a p c -> p a c"),
             )
 
-        def load_gate_scales(queue, g, q):
-            queue.dma_start(
-                out=gate_s[g][:].bitcast(I32)[32 * q : 32 * q + 4, :],
-                in_=(gl_scales, gr_scales)[g].bitcast(I32)[:, 4 * q : 4 * q + 4, :].rearrange("a r c -> r a c"),
-            )
+        def load_gate_scales(g, quadrants):
+            for q in quadrants:
+                nc.sync.dma_start(
+                    out=gate_s[g][:].bitcast(I32)[32 * q : 32 * q + 4, :],
+                    in_=(gl_scales, gr_scales)[g].bitcast(I32)[:, 4 * q : 4 * q + 4, :].rearrange("a r c -> r a c"),
+                )
 
         nc.sync.dma_start(pick[:], offs)
+        load_gate_scales(0, (0, 1))
+        for q in range(4):
+            nc.sync.dma_start(
+                out=tab_s[:].bitcast(I32)[32 * q : 32 * q + 8, :],
+                in_=tab_scales.bitcast(I32)[:, 4 * q : 4 * q + 4, :],
+            )
         load_table(0)
-        for q in range(4):
-            nc.sync.dma_start(
-                out=tab_s[:].bitcast(I32)[32 * q : 32 * q + 4, :],
-                in_=tab_scales.bitcast(I32)[:, 4 * q : 4 * q + 4, :].rearrange("a r t -> r a t"),
-            )
-        load_table(1)
-        load_raw(0, 0)
-        load_raw(0, 1)
+        load_gate_scales(0, (2, 3))
         load_gate_words(0)
-        load_gate_words(1)
-        for q in range(4):
-            load_gate_scales(nc.sync, 0, q)
-        load_raw(1, 0)
-        for q in range(4):
-            load_gate_scales(nc.sync, 1, q)
-        load_raw(1, 1)
-        nc.sync.dma_start(out=wo_w[:], in_=wo_words[0].rearrange("p c i -> p (c i)").bitcast(I32))
-        for q in range(4):
-            nc.sync.dma_start(
-                out=wo_s[:].bitcast(I32)[32 * q : 32 * q + 4, :],
-                in_=wo_scales[0].bitcast(I32)[4 * q : 4 * q + 4, :],
-            )
-        nc.sync.dma_start(place[:], offs2)
-        nc.sync.dma_start(out=wgo_sb[:], in_=wgo)
+        load_table(1)
 
-        for n in range(ROW_TILES):
-            nc.vector.memset(cache[n][:].bitcast(I32), 0)
         make_identity(nc, ident[:])
+        for n in range(ROW_TILES):
+            nc.gpsimd.memset(cache[n][:], 0.0)
 
-        def entries(h):
-            return pick[:, h * (HALF // 16) : (h + 1) * (HALF // 16)]
+        def entries(tile, h):
+            return tile[:, h * (HALF // 16) : (h + 1) * (HALF // 16)]
 
-        def gather_words(words, h, a):
-            nc.vector.tensor_copy(words[:, a, :], tab_w[a][:].bitcast(U32).indirect(entries(h)))
+        nc.vector.tensor_copy(v_s[0][:], tab_s[:].indirect(pick[:]))
+        nc.sync.dma_start(out=v_s[1][:].bitcast(I32)[0:100, :], in_=v_s[0][:].bitcast(I32)[4:104, :])
+        load_raw(0, 0, "tab_s")
+        gate_w.append(shared.tile([P, PASSES * 2 * H], U8, name="gate_w1", align_bytes=64, offset=64))
+        gate_s.append(shared.tile([P, PASSES * H], U8, name="gate_s1", align_bytes=64, offset=2112))
+        load_gate_words(1)
+        load_gate_scales(1, range(4))
+        nc.sync.dma_start(place[:], offs2)
 
-        def gather_scales(h):
-            for a in range(PASSES):
-                nc.vector.tensor_copy(v_s[a][h][:], tab_s[:, a * T : (a + 1) * T].indirect(entries(h)))
+        for a in range(PASSES):
+            for h in range(2):
+                nc.vector.tensor_copy(v_w[h][a][:], tab_w[a][:].bitcast(U32).indirect(entries(pick, h)))
+        load_raw(0, 1, "tab_w0")
+        load_raw(1, 0, "tab_w1")
 
-        def quantise_weight(g, a, tag):
-            woven = keep.tile([P, H, 4], BF16, name="woven", tag=tag, align_bytes=64)
-            dst = woven[:].rearrange("p (c i) j -> p c j i", i=4)
-            src = raw[g][a][:].rearrange("p j (c i) -> p c j i", i=4)
-            if (g, a) != (1, 1):
-                nc.scalar.copy(dst, src)
-            else:
-                nc.vector.tensor_copy(dst, src)
+        def weave(engine_copy, g, a):
+            woven = held([P, H, 4], BF16, "woven%d%d" % (g, a))
+            engine_copy(
+                woven[:].rearrange("p (c i) j -> p c j i", i=4),
+                raw[g, a][:].rearrange("p j (c i) -> p c j i", i=4),
+            )
+            return woven
+
+        def quantise_weight(g, a, woven):
             nc.vector.quantize_mx(
                 out=proj_w[g][a][:].bitcast(FP8X4),
                 scales=proj_s[g][a][:],
@@ -136,8 +133,8 @@ def tile_list_gated_pair_terms_kernel(
             for a in range(PASSES):
                 nc.tensor.matmul_mx(
                     out=bank[:],
-                    lhsT=v_w[h][:, a, j : j + P].bitcast(FP8X4),
-                    lhsT_scale=v_s[a][h][:, j : j + P],
+                    lhsT=v_w[h][a][:, j : j + P].bitcast(FP8X4),
+                    lhsT_scale=v_s[a][:, i * P : (i + 1) * P],
                     rhs=words(a),
                     rhs_scale=scales(a),
                     start=(a == 0),
@@ -153,9 +150,62 @@ def tile_list_gated_pair_terms_kernel(
         h_cols = [held([P, HALF * 4], BF16, "h_cols%d" % h) for h in range(2)]
         h_w = [held([P, HALF], U32, "h_w%d" % h) for h in range(2)]
         h_s = [held([P, HALF], U8, "h_s%d" % h) for h in range(2)]
+        sig = [[held([P, 2, H], F32, "sig%d%d" % (g, c))[:] for c in range(2)] for g in range(2)]
 
-        def out_project(h, n, y):
-            bank = psum.tile([P, HALF], F32, name="y_bank", tag="wide", bufs=3)
+        wide_used = []
+        proj_used = []
+
+        def wide_bank(shape):
+            wide_used.append(psum.tile(shape, F32, name="wide", tag="wide%d" % (len(wide_used) % 5)))
+            return wide_used[-1]
+
+        def proj_bank():
+            proj_used.append(psum.tile([P, H], F32, name="proj", tag="proj%d" % (len(proj_used) % 3)))
+            return proj_used[-1]
+
+        def gate(g, c):
+            for ii in range(2):
+                bank = wide_bank([P, H])
+                project(
+                    bank, 2 * c + ii,
+                    lambda a: gate_w[g][:, 2 * H * a : 2 * H * (a + 1)].bitcast(FP4X4),
+                    lambda a: gate_s[g][:, H * a : H * (a + 1)],
+                )
+                nc.scalar.activation(in_order(sig[g][c][:, ii, :]), from_bank(bank), SIGMOID)
+
+        gates = {}
+
+        def both_gates(c, into):
+            gates[c] = into
+            nc.vector.tensor_tensor(into, sig[0][c], sig[1][c], MULT)
+
+        def times_left(c):
+            for ii in range(2):
+                left = proj_bank()
+                project(left, 2 * c + ii, lambda a: proj_w[0][a][:].bitcast(FP8X4), lambda a: proj_s[0][a][:])
+                nc.vector.tensor_tensor(in_order(sig[1][c][:, ii, :]), from_bank(left), in_order(gates[c][:, ii, :]), MULT)
+
+        def times_right(c):
+            turned = wide_bank([P, 4, P])
+            for ii in range(2):
+                right = proj_bank()
+                project(right, 2 * c + ii, lambda a: proj_w[1][a][:].bitcast(FP8X4), lambda a: proj_s[1][a][:])
+                h_rows = held([P, H], BF16, "h_rows%d" % (2 * c + ii))
+                nc.vector.tensor_tensor(in_order(h_rows[:]), from_bank(right), in_order(sig[1][c][:, ii, :]), MULT)
+                for u in range(2):
+                    nc.tensor.transpose(turned[:, 2 * ii + u, :], h_rows[:].bitcast(F32)[:, P * u : P * (u + 1)], ident[:])
+            h, cc = divmod(c, 2)
+            nc.scalar.copy(
+                h_cols[h][:].bitcast(F32)[:, cc * 2 * CHUNK : (cc + 1) * 2 * CHUNK].rearrange("p (i t u) -> p i t u", i=2, u=2),
+                turned[:].rearrange("p (i u) t -> p i t u", u=2),
+            )
+
+        def quantise_h(h):
+            nc.vector.quantize_mx(out=h_w[h][:].bitcast(FP8X4), scales=h_s[h][:], in_=h_cols[h][:])
+
+        def out_project(h, n, tag):
+            y = held([P, HALF], F32, "y%d%d" % (h, n), tag)
+            bank = wide_bank([P, HALF])
             nc.tensor.matmul_mx(
                 out=bank[:],
                 lhsT=wo_w[:, n * P : (n + 1) * P].bitcast(FP8X4),
@@ -165,97 +215,62 @@ def tile_list_gated_pair_terms_kernel(
                 start=True,
                 stop=True,
             )
-            nc.scalar.copy(y, bank[:])
+            nc.scalar.copy(y[:], bank[:])
             return y
 
         def scatter(h, n, y):
             nc.vector.tensor_tensor(
-                cache[n][:].indirect(place[:, h * (HALF // 16) : (h + 1) * (HALF // 16)]),
-                y, wgo_sb[:, h * HALF : (h + 1) * HALF], MULT,
+                cache[n][:].indirect(entries(place, h)), y[:], wgo_sb[:, h * HALF : (h + 1) * HALF], MULT,
             )
 
-        def pair(name, tag):
-            return keep.tile([P, 2, H], F32, name=name, tag=tag, align_bytes=64)[:]
-
-        def gate(g, c, sig):
-            for ii in range(2):
-                bank = psum.tile([P, H], F32, name="gate_bank", tag="wide", bufs=3)
-                project(
-                    bank, 2 * c + ii,
-                    lambda a: gate_w[g][:, 2 * H * a : 2 * H * (a + 1)].bitcast(FP4X4),
-                    lambda a: gate_s[g][:, H * a : H * (a + 1)],
-                )
-                nc.scalar.activation(in_order(sig[:, ii, :]), from_bank(bank), SIGMOID)
-            return sig
-
-        def gated_left(c, sig):
-            once = pair("once", "once%d" % c)
-            for ii in range(2):
-                left = psum.tile([P, H], F32, name="left", tag="proj", bufs=3)
-                project(left, 2 * c + ii, lambda a: proj_w[0][a][:].bitcast(FP8X4), lambda a: proj_s[0][a][:])
-                nc.vector.tensor_tensor(in_order(once[:, ii, :]), from_bank(left), in_order(sig[:, ii, :]), MULT)
-            return once
-
-        def gated_twice(c, once, sig, tag):
-            twice = pair("twice", tag)
-            nc.vector.tensor_tensor(twice, once, sig, MULT)
-            return twice
-
-        def times_right(c, gated):
-            turned = psum.tile([P, 4, P], F32, name="turned", bufs=2)
-            for ii in range(2):
-                right = psum.tile([P, H], F32, name="right", tag="proj", bufs=3)
-                project(right, 2 * c + ii, lambda a: proj_w[1][a][:].bitcast(FP8X4), lambda a: proj_s[1][a][:])
-                h_rows = keep.tile([P, H], BF16, name="h_rows", tag="h_rows%d" % (2 * c + ii))
-                nc.vector.tensor_tensor(in_order(h_rows[:]), from_bank(right), in_order(gated[:, ii, :]), MULT)
-                for u in range(2):
-                    nc.tensor.transpose(turned[:, 2 * ii + u, :], h_rows[:].bitcast(F32)[:, P * u : P * (u + 1)], ident[:])
-            h, cc = divmod(c, 2)
-            nc.scalar.copy(
-                h_cols[h][:].bitcast(F32)[:, cc * 2 * CHUNK : (cc + 1) * 2 * CHUNK].rearrange("p (i t u) -> p i t u", i=2, u=2),
-                turned[:].rearrange("p (i u) t -> p i t u", u=2),
+        gate(0, 0)
+        gate(0, 1)
+        quantise_weight(0, 0, weave(nc.vector.tensor_copy, 0, 0))
+        load_raw(1, 1, "tab_s")
+        wo_w = held([P, N], I32, "wo_w", "woven00")
+        nc.sync.dma_start(out=wo_w[:], in_=wo_words[0].rearrange("p c i -> p (c i)").bitcast(I32))
+        gate(1, 0)
+        gate(1, 1)
+        quantise_weight(0, 1, weave(nc.vector.tensor_copy, 0, 1))
+        wgo_sb = held([P, S], F32, "wgo_sb", "tab_w0")
+        nc.sync.dma_start(out=wgo_sb[:], in_=wgo)
+        early = held([P, 2, 2, H], F32, "early", "woven01")
+        both_gates(0, early[:, 0])
+        both_gates(1, early[:, 1])
+        wo_s = held([P, N], U8, "wo_s", "sig00")
+        for q in range(4):
+            nc.sync.dma_start(
+                out=wo_s[:].bitcast(I32)[32 * q : 32 * q + 4, :],
+                in_=wo_scales[0].bitcast(I32)[4 * q : 4 * q + 4, :],
             )
-            if cc == 1:
-                nc.vector.quantize_mx(out=h_w[h][:].bitcast(FP8X4), scales=h_s[h][:], in_=h_cols[h][:])
-
-        v_w = [held([P, PASSES, HALF], U32, "v_w0")]
-        gather_words(v_w[0], 0, 0)
-        gather_scales(0)
-        gather_words(v_w[0], 0, 1)
-        gather_scales(1)
-        quantise_weight(0, 0, "woven00")
-        v_w.append(keep.tile([P, PASSES, HALF], U32, name="v_w1", tag="woven00", align_bytes=64))
-        for a in range(PASSES):
-            gather_words(v_w[1], 1, a)
-        quantise_weight(0, 1, "woven01")
-        sig_l0 = gate(0, 0, pair("sig_l0", "sig_l0"))
-        sig_l1 = gate(0, 1, pair("sig_l1", "sig_l1"))
-        once0 = gated_left(0, sig_l0)
-        once1 = gated_left(1, sig_l1)
-        twice0 = gated_twice(0, once0, gate(1, 0, pair("sig_r0", "sig_r0")), "twice0")
-        sig_r1 = gate(1, 1, pair("sig_r1", "sig_r1"))
-        quantise_weight(1, 0, "woven10")
-        quantise_weight(1, 1, "sig_r0")
-        twice1 = gated_twice(1, once1, sig_r1, "twice1")
-        times_right(0, twice0)
-        times_right(1, twice1)
-        late = keep.tile([P, 2, 2, H], F32, name="late", tag="raw10", align_bytes=64)
-        once2 = gated_left(2, gate(0, 2, late[:, 0]))
-        twice2 = gated_twice(2, once2, gate(1, 2, late[:, 1]), "twice2")
-        y_first = keep.tile([P, HALF], F32, name="y_first", tag="twice3", align_bytes=64)
-        out_project(0, 0, y_first[:])
-        times_right(2, twice2)
-        once3 = gated_left(3, gate(0, 3, pair("sig_l3", "sig_l0")))
-        sig_r3 = gate(1, 3, pair("sig_r3", "sig_l1"))
-        scatter(0, 0, y_first[:])
-        times_right(3, gated_twice(3, once3, sig_r3, "twice3"))
-        y_second = keep.tile([P, HALF], F32, name="y_second", tag="once3", align_bytes=64)
-        scatter(0, 1, out_project(0, 1, y_second[:]))
-        y_third = keep.tile([P, HALF], F32, name="y_third", tag="h_rows7")
-        scatter(0, 2, out_project(0, 2, y_third[:]))
-        y_last = held([P, ROW_TILES, HALF], F32, "y_last")
+        times_left(0)
+        times_left(1)
+        quantise_weight(1, 0, weave(nc.scalar.copy, 1, 0))
+        quantise_weight(1, 1, weave(nc.scalar.copy, 1, 1))
+        third = held([P, 2, 2, H], F32, "third", "tab_w1")
+        fourth = shared.tile([P, 2, 2, H], F32, name="fourth", align_bytes=64, offset=3136)
+        for g in range(2):
+            sig[g].extend([third[:, g], fourth[:, g]])
+        gate(0, 2)
+        gate(1, 2)
+        gate(0, 3)
+        times_right(0)
+        gate(1, 3)
+        times_right(1)
+        both_gates(2, held([P, 2, H], F32, "gates2", "sig10")[:])
+        times_left(2)
+        quantise_h(0)
+        both_gates(3, held([P, 2, H], F32, "gates3", "sig11")[:])
+        times_left(3)
+        y_first = out_project(0, 0, None)
+        times_right(2)
+        scatter(0, 0, y_first)
+        times_right(3)
+        scatter(0, 1, out_project(0, 1, "h_rows7"))
+        quantise_h(1)
+        scatter(0, 2, out_project(0, 2, "h_cols1"))
         for n in range(ROW_TILES):
-            scatter(1, n, out_project(1, n, y_last[:, n, :]))
+            scatter(1, n, out_project(1, n, None))
         for n in range(ROW_TILES):
             for queue, cols in ((nc.sync, slice(0, T2 // 2)), (nc.scalar, slice(T2 // 2, T2))):
                 queue.dma_start(out=out[n * P : (n + 1) * P, cols], in_=cache[n][:, cols])

@@ -148,24 +148,20 @@ def tile_list_gated_pair_terms_kernel(
             return tile.rearrange("t (u p e) -> t u p e", u=2, e=2)
 
         h_cols = [held([P, HALF * 4], BF16, "h_cols%d" % h) for h in range(2)]
-        h_w = [held([P, HALF], U32, "h_w%d" % h) for h in range(2)]
+        h_w = {}
         h_s = [held([P, HALF], U8, "h_s%d" % h) for h in range(2)]
-        sig = [[held([P, 2, H], F32, "sig%d%d" % (g, c))[:] for c in range(2)] for g in range(2)]
+        sig = [[held([P, 2, H], F32, "sig%d%d" % (g, c)) for c in range(4)] for g in range(2)]
+        banks_used = []
+        gates = {}
+        h_rows = {}
 
-        wide_used = []
-        proj_used = []
-
-        def wide_bank(shape):
-            wide_used.append(psum.tile(shape, F32, name="wide", tag="wide%d" % (len(wide_used) % 5)))
-            return wide_used[-1]
-
-        def proj_bank():
-            proj_used.append(psum.tile([P, H], F32, name="proj", tag="proj%d" % (len(proj_used) % 3)))
-            return proj_used[-1]
+        def next_bank(shape):
+            banks_used.append(psum.tile(shape, F32, name="bank", tag="bank%d" % (len(banks_used) % 8)))
+            return banks_used[-1]
 
         def gate(g, c):
             for ii in range(2):
-                bank = wide_bank([P, H])
+                bank = next_bank([P, H])
                 project(
                     bank, 2 * c + ii,
                     lambda a: gate_w[g][:, 2 * H * a : 2 * H * (a + 1)].bitcast(FP4X4),
@@ -173,39 +169,43 @@ def tile_list_gated_pair_terms_kernel(
                 )
                 nc.scalar.activation(in_order(sig[g][c][:, ii, :]), from_bank(bank), SIGMOID)
 
-        gates = {}
-
-        def both_gates(c, into):
+        def both_gates(c, into, engine):
             gates[c] = into
-            nc.vector.tensor_tensor(into, sig[0][c], sig[1][c], MULT)
+            engine.tensor_tensor(into, sig[0][c][:], sig[1][c][:], MULT)
 
-        def times_left(c):
+        def projection(g, c):
+            banks = [next_bank([P, H]) for ii in range(2)]
             for ii in range(2):
-                left = proj_bank()
-                project(left, 2 * c + ii, lambda a: proj_w[0][a][:].bitcast(FP8X4), lambda a: proj_s[0][a][:])
-                nc.vector.tensor_tensor(in_order(sig[1][c][:, ii, :]), from_bank(left), in_order(gates[c][:, ii, :]), MULT)
+                project(banks[ii], 2 * c + ii, lambda a: proj_w[g][a][:].bitcast(FP8X4), lambda a: proj_s[g][a][:])
+            return banks
 
-        def times_right(c):
-            turned = wide_bank([P, 4, P])
+        def times_left(c, left):
             for ii in range(2):
-                right = proj_bank()
-                project(right, 2 * c + ii, lambda a: proj_w[1][a][:].bitcast(FP8X4), lambda a: proj_s[1][a][:])
-                h_rows = held([P, H], BF16, "h_rows%d" % (2 * c + ii))
-                nc.vector.tensor_tensor(in_order(h_rows[:]), from_bank(right), in_order(sig[1][c][:, ii, :]), MULT)
+                nc.vector.tensor_tensor(in_order(sig[1][c][:, ii, :]), from_bank(left[ii]), in_order(gates[c][:, ii, :]), MULT)
+
+        def times_right(c, right):
+            for ii in range(2):
+                h_rows[c, ii] = held([P, H], BF16, "h_rows%d%d" % (c, ii))
+                nc.vector.tensor_tensor(in_order(h_rows[c, ii][:]), from_bank(right[ii]), in_order(sig[1][c][:, ii, :]), MULT)
+
+        def turn(c):
+            turned = next_bank([P, 4, P])
+            for ii in range(2):
                 for u in range(2):
-                    nc.tensor.transpose(turned[:, 2 * ii + u, :], h_rows[:].bitcast(F32)[:, P * u : P * (u + 1)], ident[:])
+                    nc.tensor.transpose(turned[:, 2 * ii + u, :], h_rows[c, ii][:].bitcast(F32)[:, P * u : P * (u + 1)], ident[:])
             h, cc = divmod(c, 2)
             nc.scalar.copy(
                 h_cols[h][:].bitcast(F32)[:, cc * 2 * CHUNK : (cc + 1) * 2 * CHUNK].rearrange("p (i t u) -> p i t u", i=2, u=2),
                 turned[:].rearrange("p (i u) t -> p i t u", u=2),
             )
 
-        def quantise_h(h):
+        def quantise_h(h, tag):
+            h_w[h] = held([P, HALF], U32, "h_w%d" % h, tag)
             nc.vector.quantize_mx(out=h_w[h][:].bitcast(FP8X4), scales=h_s[h][:], in_=h_cols[h][:])
 
         def out_project(h, n, tag):
             y = held([P, HALF], F32, "y%d%d" % (h, n), tag)
-            bank = wide_bank([P, HALF])
+            bank = next_bank([P, HALF])
             nc.tensor.matmul_mx(
                 out=bank[:],
                 lhsT=wo_w[:, n * P : (n + 1) * P].bitcast(FP8X4),
@@ -223,51 +223,53 @@ def tile_list_gated_pair_terms_kernel(
                 cache[n][:].indirect(entries(place, h)), y[:], wgo_sb[:, h * HALF : (h + 1) * HALF], MULT,
             )
 
-        gate(0, 0)
-        gate(0, 1)
+        for c in range(4):
+            gate(0, c)
         quantise_weight(0, 0, weave(nc.vector.tensor_copy, 0, 0))
         load_raw(1, 1, "tab_s")
         wo_w = held([P, N], I32, "wo_w", "woven00")
         nc.sync.dma_start(out=wo_w[:], in_=wo_words[0].rearrange("p c i -> p (c i)").bitcast(I32))
-        gate(1, 0)
-        gate(1, 1)
         quantise_weight(0, 1, weave(nc.vector.tensor_copy, 0, 1))
         wgo_sb = held([P, S], F32, "wgo_sb", "tab_w0")
         nc.sync.dma_start(out=wgo_sb[:], in_=wgo)
-        early = held([P, 2, 2, H], F32, "early", "woven01")
-        both_gates(0, early[:, 0])
-        both_gates(1, early[:, 1])
-        wo_s = held([P, N], U8, "wo_s", "sig00")
+        wo_s = held([P, N], U8, "wo_s", "woven01")
         for q in range(4):
             nc.sync.dma_start(
                 out=wo_s[:].bitcast(I32)[32 * q : 32 * q + 4, :],
                 in_=wo_scales[0].bitcast(I32)[4 * q : 4 * q + 4, :],
             )
-        times_left(0)
-        times_left(1)
-        quantise_weight(1, 0, weave(nc.scalar.copy, 1, 0))
-        quantise_weight(1, 1, weave(nc.scalar.copy, 1, 1))
-        third = held([P, 2, 2, H], F32, "third", "tab_w1")
-        fourth = shared.tile([P, 2, 2, H], F32, name="fourth", align_bytes=64, offset=3136)
-        for g in range(2):
-            sig[g].extend([third[:, g], fourth[:, g]])
-        gate(0, 2)
-        gate(1, 2)
-        gate(0, 3)
-        times_right(0)
-        gate(1, 3)
-        times_right(1)
-        both_gates(2, held([P, 2, H], F32, "gates2", "sig10")[:])
-        times_left(2)
-        quantise_h(0)
-        both_gates(3, held([P, 2, H], F32, "gates3", "sig11")[:])
-        times_left(3)
+        for c in range(4):
+            gate(1, c)
+        woven = weave(nc.vector.tensor_copy, 1, 0)
+        both_gates(0, held([P, 2, H], F32, "gates0", "tab_w1")[:], nc.vector)
+        quantise_weight(1, 0, woven)
+        quantise_weight(1, 1, weave(nc.vector.tensor_copy, 1, 1))
+        later = held([P, 3, 2, H], F32, "later", "woven11")
+        for c in range(1, 4):
+            both_gates(c, later[:, c - 1], nc.gpsimd)
+        left = [projection(0, c) for c in range(3)]
+        right = [projection(1, 0)]
+        times_left(0, left[0])
+        times_right(0, right[0])
+        right.append(projection(1, 1))
+        times_left(1, left[1])
+        turn(0)
+        times_right(1, right[1])
+        times_left(2, left[2])
+        left.append(projection(0, 3))
+        turn(1)
+        right.append(projection(1, 2))
+        times_right(2, right[2])
+        quantise_h(0, "sig12")
+        right.append(projection(1, 3))
+        times_left(3, left[3])
         y_first = out_project(0, 0, None)
-        times_right(2)
+        times_right(3, right[3])
+        turn(2)
+        turn(3)
         scatter(0, 0, y_first)
-        times_right(3)
-        scatter(0, 1, out_project(0, 1, "h_rows7"))
-        quantise_h(1)
+        quantise_h(1, None)
+        scatter(0, 1, out_project(0, 1, "h_rows31"))
         scatter(0, 2, out_project(0, 2, "h_cols1"))
         for n in range(ROW_TILES):
             scatter(1, n, out_project(1, n, None))

@@ -38,11 +38,14 @@ def tile_list_gated_pair_terms_kernel(
         def held(shape, dtype, name, tag=None):
             return keep.tile(shape, dtype, name=name, tag=tag or name, align_bytes=64)
 
+        def placed(shape, dtype, name, offset):
+            return shared.tile(shape, dtype, name=name, align_bytes=64, offset=offset)
+
         pick = lists.tile([P, S // 16], U16, name="pick")
         place = lists.tile([P, S // 16], U16, name="place")
 
-        tab_w = [held([P, T], I32, "tab_w%d" % a) for a in range(PASSES)]
-        tab_s = shared.tile([P, T], U8, name="tab_s", align_bytes=64, offset=2048)
+        tab_w = [placed([P, T], I32, "tab_w0", 4096), held([P, T], I32, "tab_w1")]
+        tab_s = placed([P, T], U8, "tab_s", 20480)
         v_w = [[held([P, HALF], U32, "v_w%d%d" % (h, a)) for a in range(PASSES)] for h in range(2)]
         v_s = [held([P, S], U8, "v_s%d" % a) for a in range(PASSES)]
         gate_w = [held([P, PASSES * 2 * H], U8, "gate_w0")]
@@ -55,12 +58,9 @@ def tile_list_gated_pair_terms_kernel(
 
         nc.gpsimd.memset(tab_s[:].bitcast(I32), 0)
 
-        def load_raw(g, a, tag):
+        def load_raw(g, a, tile):
             w = (wl, wr)[g]
-            if g == a:
-                raw[g, a] = shared.tile([P, 4, H], F32, name="raw%d%d" % (g, a), align_bytes=64, offset=3136)
-            else:
-                raw[g, a] = held([P, 4, H], F32, "raw%d%d" % (g, a), tag)
+            raw[g, a] = tile
             nc.sync.dma_start(out=raw[g, a][:], in_=w[512 * a : 512 * (a + 1), :].rearrange("(p j) c -> p j c", j=4))
 
         def load_table(a):
@@ -100,9 +100,9 @@ def tile_list_gated_pair_terms_kernel(
 
         nc.vector.tensor_copy(v_s[0][:], tab_s[:].indirect(pick[:]))
         nc.sync.dma_start(out=v_s[1][:].bitcast(I32)[0:100, :], in_=v_s[0][:].bitcast(I32)[4:104, :])
-        load_raw(0, 0, "tab_s")
-        gate_w.append(shared.tile([P, PASSES * 2 * H], U8, name="gate_w1", align_bytes=64, offset=64))
-        gate_s.append(shared.tile([P, PASSES * H], U8, name="gate_s1", align_bytes=64, offset=2112))
+        load_raw(0, 0, placed([P, 4, H], F32, "raw00", 21568))
+        gate_w.append(placed([P, PASSES * 2 * H], U8, "gate_w1", 18496))
+        gate_s.append(placed([P, PASSES * H], U8, "gate_s1", 20544))
         load_gate_words(1)
         load_gate_scales(1, range(4))
         nc.sync.dma_start(place[:], offs2)
@@ -110,11 +110,11 @@ def tile_list_gated_pair_terms_kernel(
         for a in range(PASSES):
             for h in range(2):
                 nc.vector.tensor_copy(v_w[h][a][:], tab_w[a][:].bitcast(U32).indirect(entries(pick, h)))
-        load_raw(0, 1, "tab_w0")
-        load_raw(1, 0, "tab_w1")
+        load_raw(0, 1, placed([P, 4, H], F32, "raw01", 5184))
+        load_raw(1, 0, held([P, 4, H], F32, "raw10", "tab_w1"))
 
-        def weave(engine_copy, g, a):
-            woven = held([P, H, 4], BF16, "woven%d%d" % (g, a))
+        def weave(engine_copy, g, a, woven=None):
+            woven = held([P, H, 4], BF16, "woven%d%d" % (g, a)) if woven is None else woven
             engine_copy(
                 woven[:].rearrange("p (c i) j -> p c j i", i=4),
                 raw[g, a][:].rearrange("p j (c i) -> p c j i", i=4),
@@ -150,46 +150,43 @@ def tile_list_gated_pair_terms_kernel(
         h_cols = [held([P, HALF * 4], BF16, "h_cols%d" % h) for h in range(2)]
         h_w = {}
         h_s = [held([P, HALF], U8, "h_s%d" % h) for h in range(2)]
-        sig = [[held([P, 2, H], F32, "sig%d%d" % (g, c)) for c in range(4)] for g in range(2)]
-        banks_used = []
-        gates = {}
+        sig = {}
         h_rows = {}
 
-        def next_bank(shape):
-            banks_used.append(psum.tile(shape, F32, name="bank", tag="bank%d" % (len(banks_used) % 8)))
-            return banks_used[-1]
+        def bank_tile(b, shape):
+            return psum.tile(shape, F32, name="bank", tag="bank%d" % b)
 
-        def gate(g, c):
+        def gate(g, c, b, into):
+            sig[g, c] = into
             for ii in range(2):
-                bank = next_bank([P, H])
+                bank = bank_tile(b + ii, [P, H])
                 project(
                     bank, 2 * c + ii,
                     lambda a: gate_w[g][:, 2 * H * a : 2 * H * (a + 1)].bitcast(FP4X4),
                     lambda a: gate_s[g][:, H * a : H * (a + 1)],
                 )
-                nc.scalar.activation(in_order(sig[g][c][:, ii, :]), from_bank(bank), SIGMOID)
+                nc.scalar.activation(in_order(into[:, ii, :]), from_bank(bank), SIGMOID)
 
-        def both_gates(c, into, engine):
-            gates[c] = into
-            engine.tensor_tensor(into, sig[0][c][:], sig[1][c][:], MULT)
-
-        def projection(g, c):
-            banks = [next_bank([P, H]) for ii in range(2)]
+        def projection(g, c, b):
+            banks = [bank_tile(b + ii, [P, H]) for ii in range(2)]
             for ii in range(2):
                 project(banks[ii], 2 * c + ii, lambda a: proj_w[g][a][:].bitcast(FP8X4), lambda a: proj_s[g][a][:])
             return banks
 
-        def times_left(c, left):
-            for ii in range(2):
-                nc.vector.tensor_tensor(in_order(sig[1][c][:, ii, :]), from_bank(left[ii]), in_order(gates[c][:, ii, :]), MULT)
+        def pair(name, tag=None):
+            return held([P, 2, H], F32, name, tag)[:]
 
-        def times_right(c, right):
+        def times_left(left, factor, into):
+            for ii in range(2):
+                nc.vector.tensor_tensor(in_order(into[:, ii, :]), from_bank(left[ii]), in_order(factor[:, ii, :]), MULT)
+
+        def times_right(c, right, factor):
             for ii in range(2):
                 h_rows[c, ii] = held([P, H], BF16, "h_rows%d%d" % (c, ii))
-                nc.vector.tensor_tensor(in_order(h_rows[c, ii][:]), from_bank(right[ii]), in_order(sig[1][c][:, ii, :]), MULT)
+                nc.vector.tensor_tensor(in_order(h_rows[c, ii][:]), from_bank(right[ii]), in_order(factor[ii]), MULT)
 
-        def turn(c):
-            turned = next_bank([P, 4, P])
+        def turn(c, b):
+            turned = bank_tile(b, [P, 4, P])
             for ii in range(2):
                 for u in range(2):
                     nc.tensor.transpose(turned[:, 2 * ii + u, :], h_rows[c, ii][:].bitcast(F32)[:, P * u : P * (u + 1)], ident[:])
@@ -199,13 +196,12 @@ def tile_list_gated_pair_terms_kernel(
                 turned[:].rearrange("p (i u) t -> p i t u", u=2),
             )
 
-        def quantise_h(h, tag):
-            h_w[h] = held([P, HALF], U32, "h_w%d" % h, tag)
+        def quantise_h(h, words):
+            h_w[h] = words
             nc.vector.quantize_mx(out=h_w[h][:].bitcast(FP8X4), scales=h_s[h][:], in_=h_cols[h][:])
 
-        def out_project(h, n, tag):
-            y = held([P, HALF], F32, "y%d%d" % (h, n), tag)
-            bank = next_bank([P, HALF])
+        def out_project(h, n, y, b):
+            bank = bank_tile(b, [P, HALF])
             nc.tensor.matmul_mx(
                 out=bank[:],
                 lhsT=wo_w[:, n * P : (n + 1) * P].bitcast(FP8X4),
@@ -224,13 +220,13 @@ def tile_list_gated_pair_terms_kernel(
             )
 
         for c in range(4):
-            gate(0, c)
+            gate(0, c, 2 * c, pair("sig0%d" % c))
         quantise_weight(0, 0, weave(nc.vector.tensor_copy, 0, 0))
-        load_raw(1, 1, "tab_s")
+        load_raw(1, 1, placed([P, 4, H], F32, "raw11", 21568))
         wo_w = held([P, N], I32, "wo_w", "woven00")
         nc.sync.dma_start(out=wo_w[:], in_=wo_words[0].rearrange("p c i -> p (c i)").bitcast(I32))
         quantise_weight(0, 1, weave(nc.vector.tensor_copy, 0, 1))
-        wgo_sb = held([P, S], F32, "wgo_sb", "tab_w0")
+        wgo_sb = placed([P, S], F32, "wgo_sb", 5184)
         nc.sync.dma_start(out=wgo_sb[:], in_=wgo)
         wo_s = held([P, N], U8, "wo_s", "woven01")
         for q in range(4):
@@ -238,41 +234,51 @@ def tile_list_gated_pair_terms_kernel(
                 out=wo_s[:].bitcast(I32)[32 * q : 32 * q + 4, :],
                 in_=wo_scales[0].bitcast(I32)[4 * q : 4 * q + 4, :],
             )
-        for c in range(4):
-            gate(1, c)
-        woven = weave(nc.vector.tensor_copy, 1, 0)
-        both_gates(0, held([P, 2, H], F32, "gates0", "tab_w1")[:], nc.vector)
-        quantise_weight(1, 0, woven)
-        quantise_weight(1, 1, weave(nc.vector.tensor_copy, 1, 1))
-        later = held([P, 3, 2, H], F32, "later", "woven11")
-        for c in range(1, 4):
-            both_gates(c, later[:, c - 1], nc.gpsimd)
-        left = [projection(0, c) for c in range(3)]
-        right = [projection(1, 0)]
-        times_left(0, left[0])
-        times_right(0, right[0])
-        right.append(projection(1, 1))
-        times_left(1, left[1])
-        turn(0)
-        times_right(1, right[1])
-        times_left(2, left[2])
-        left.append(projection(0, 3))
-        turn(1)
-        right.append(projection(1, 2))
-        times_right(2, right[2])
-        quantise_h(0, "sig12")
-        right.append(projection(1, 3))
-        times_left(3, left[3])
-        y_first = out_project(0, 0, None)
-        times_right(3, right[3])
-        turn(2)
-        turn(3)
+        for c in range(2):
+            gate(1, c, 2 * c, pair("sig1%d" % c))
+        first_pass = weave(nc.vector.tensor_copy, 1, 0)
+        gates0 = pair("gates0", "tab_w1")
+        nc.vector.tensor_tensor(gates0, sig[0, 0], sig[1, 0], MULT)
+        quantise_weight(1, 0, first_pass)
+        second_pass = weave(nc.scalar.copy, 1, 1, held([P, H, 4], BF16, "woven11", "sig10"))
+        late_sigs = placed([P, 2, 2, H], F32, "late_sigs", 21568)
+        for c in range(2, 4):
+            gate(1, c, 2 * c, late_sigs[:, c - 2])
+        gates1 = pair("gates1", "woven10")
+        nc.gpsimd.tensor_tensor(gates1, sig[0, 1], sig[1, 1], MULT)
+        left = {0: projection(0, 0, 0), 2: projection(0, 2, 2)}
+        twice = {c: pair("twice%d" % c) for c in (0, 1, 3)}
+        times_left(left[0], gates0, twice[0])
+        once2 = pair("once2", "sig00")
+        times_left(left[2], sig[0, 2], once2)
+        left[1] = projection(0, 1, 0)
+        quantise_weight(1, 1, second_pass)
+        later = held([P, 2, 2, H], F32, "later", "sig10")
+        twice[2] = later[:, 0]
+        gates3 = later[:, 1]
+        nc.gpsimd.tensor_tensor(twice[2], once2, sig[1, 2], MULT)
+        nc.gpsimd.tensor_tensor(gates3, sig[0, 3], sig[1, 3], MULT)
+        right = [projection(1, c, 2 + 2 * c) for c in range(3)]
+        times_left(left[1], gates1, twice[1])
+        times_right(0, right[0], (twice[0][:, 0], twice[0][:, 1]))
+        turn(0, 2)
+        times_right(1, right[1], (twice[1][:, 0], twice[1][:, 1]))
+        turn(1, 4)
+        left[3] = projection(0, 3, 0)
+        times_right(2, right[2], (twice[2][:, 0], twice[2][:, 1]))
+        quantise_h(0, placed([P, HALF], U32, "h_w0", 21568))
+        y_first = out_project(0, 0, held([P, HALF], F32, "y00"), 3)
+        right.append(projection(1, 3, 6))
+        times_left(left[3], gates3, twice[3])
+        turn(2, 5)
+        times_right(3, right[3], (twice[3][:, 0], twice[3][:, 1]))
+        turn(3, 0)
         scatter(0, 0, y_first)
-        quantise_h(1, None)
-        scatter(0, 1, out_project(0, 1, "h_rows31"))
-        scatter(0, 2, out_project(0, 2, "h_cols1"))
+        quantise_h(1, held([P, HALF], U32, "h_w1"))
+        scatter(0, 1, out_project(0, 1, held([P, HALF], F32, "y01", "h_rows31"), 1))
+        scatter(0, 2, out_project(0, 2, held([P, HALF], F32, "y02", "h_cols1"), 2))
         for n in range(ROW_TILES):
-            scatter(1, n, out_project(1, n, None))
+            scatter(1, n, out_project(1, n, held([P, HALF], F32, "y1%d" % n), 3 + n))
         for n in range(ROW_TILES):
             for queue, cols in ((nc.sync, slice(0, T2 // 2)), (nc.scalar, slice(T2 // 2, T2))):
                 queue.dma_start(out=out[n * P : (n + 1) * P, cols], in_=cache[n][:, cols])

@@ -22,6 +22,9 @@ PASSES = K // 512
 HALF = S // 2
 CHUNK = 256
 ROW_TILES = N // P
+LEFT, RIGHT = 0, 1
+
+BELOW, TABLE_SCALES, ABOVE = 0, T // 2, T
 
 
 def tile_list_gated_pair_terms_kernel(
@@ -32,36 +35,42 @@ def tile_list_gated_pair_terms_kernel(
     with ExitStack() as ctx:
         lists = ctx.enter_context(tc.tile_pool(name="lists", bufs=1))
         keep = ctx.enter_context(tc.tile_pool(name="keep", bufs=1))
-        shared = ctx.enter_context(tc.tile_pool(name="shared", bufs=1))
+        by_hand = ctx.enter_context(tc.tile_pool(name="by_hand", bufs=1))
         psum = ctx.enter_context(tc.psum_pool(name="psum", bufs=1))
 
-        def held(shape, dtype, name, tag=None):
-            return keep.tile(shape, dtype, name=name, tag=tag or name, align_bytes=64)
+        def held(shape, dtype, name, on=None):
+            return keep.tile(shape, dtype, name=name, tag=on or name, align_bytes=64)
 
         def placed(shape, dtype, name, offset):
-            return shared.tile(shape, dtype, name=name, align_bytes=64, offset=offset)
+            return by_hand.tile(shape, dtype, name=name, align_bytes=64, offset=offset)
+
+        def bank_tile(b, shape):
+            return psum.tile(shape, F32, name="bank", tag="bank%d" % b)
+
+        def chunk_tile(name, on=None):
+            return held([P, 2, H], F32, name, on)[:]
 
         pick = lists.tile([P, S // 16], U16, name="pick")
         place = lists.tile([P, S // 16], U16, name="place")
 
-        tab_w = [placed([P, T], I32, "tab_w0", 4096), held([P, T], I32, "tab_w1")]
-        tab_s = placed([P, T], U8, "tab_s", 20480)
+        tab_w = [held([P, T], I32, "tab_w%d" % a) for a in range(PASSES)]
+        tab_s = placed([P, T], U8, "tab_s", TABLE_SCALES)
         v_w = [[held([P, HALF], U32, "v_w%d%d" % (h, a)) for a in range(PASSES)] for h in range(2)]
         v_s = [held([P, S], U8, "v_s%d" % a) for a in range(PASSES)]
-        gate_w = [held([P, PASSES * 2 * H], U8, "gate_w0")]
-        gate_s = [held([P, PASSES * H], U8, "gate_s0")]
-        raw = {}
+        gate_w = {LEFT: held([P, PASSES * 2 * H], U8, "gate_w0")}
+        gate_s = [held([P, PASSES * H], U8, "gate_s%d" % g) for g in range(2)]
         proj_w = [[held([P, H], U32, "proj_w%d%d" % (g, a)) for a in range(PASSES)] for g in range(2)]
         proj_s = [[held([P, H], U8, "proj_s%d%d" % (g, a)) for a in range(PASSES)] for g in range(2)]
         cache = [held([P, T2], F32, "cache%d" % n) for n in range(ROW_TILES)]
         ident = held([P, P], F32, "ident")
-
-        nc.gpsimd.memset(tab_s[:].bitcast(I32), 0)
+        h_cols = [held([P, HALF * 4], BF16, "h_cols%d" % h) for h in range(2)]
+        h_s = [held([P, HALF], U8, "h_s%d" % h) for h in range(2)]
+        raw, sig, h_rows, h_w = {}, {}, {}, {}
 
         def load_raw(g, a, tile):
-            w = (wl, wr)[g]
             raw[g, a] = tile
-            nc.sync.dma_start(out=raw[g, a][:], in_=w[512 * a : 512 * (a + 1), :].rearrange("(p j) c -> p j c", j=4))
+            rows = (wl, wr)[g][512 * a : 512 * (a + 1), :]
+            nc.sync.dma_start(out=tile[:], in_=rows.rearrange("(p j) c -> p j c", j=4))
 
         def load_table(a):
             nc.sync.dma_start(out=tab_w[a][:], in_=tab_words[a].rearrange("p t i -> p (t i)").bitcast(I32))
@@ -79,43 +88,11 @@ def tile_list_gated_pair_terms_kernel(
                     in_=(gl_scales, gr_scales)[g].bitcast(I32)[:, 4 * q : 4 * q + 4, :].rearrange("a r c -> r a c"),
                 )
 
-        nc.sync.dma_start(pick[:], offs)
-        load_gate_scales(0, (0, 1))
-        for q in range(4):
-            nc.sync.dma_start(
-                out=tab_s[:].bitcast(I32)[32 * q : 32 * q + 8, :],
-                in_=tab_scales.bitcast(I32)[:, 4 * q : 4 * q + 4, :],
-            )
-        load_table(0)
-        load_gate_scales(0, (2, 3))
-        load_gate_words(0)
-        load_table(1)
+        def entries(offsets, h):
+            return offsets[:, h * (HALF // 16) : (h + 1) * (HALF // 16)]
 
-        make_identity(nc, ident[:])
-        for n in range(ROW_TILES):
-            nc.gpsimd.memset(cache[n][:], 0.0)
-
-        def entries(tile, h):
-            return tile[:, h * (HALF // 16) : (h + 1) * (HALF // 16)]
-
-        nc.vector.tensor_copy(v_s[0][:], tab_s[:].indirect(pick[:]))
-        nc.sync.dma_start(out=v_s[1][:].bitcast(I32)[0:100, :], in_=v_s[0][:].bitcast(I32)[4:104, :])
-        load_raw(0, 0, placed([P, 4, H], F32, "raw00", 21568))
-        gate_w.append(placed([P, PASSES * 2 * H], U8, "gate_w1", 18496))
-        gate_s.append(placed([P, PASSES * H], U8, "gate_s1", 20544))
-        load_gate_words(1)
-        load_gate_scales(1, range(4))
-        nc.sync.dma_start(place[:], offs2)
-
-        for a in range(PASSES):
-            for h in range(2):
-                nc.vector.tensor_copy(v_w[h][a][:], tab_w[a][:].bitcast(U32).indirect(entries(pick, h)))
-        load_raw(0, 1, placed([P, 4, H], F32, "raw01", 5184))
-        load_raw(1, 0, held([P, 4, H], F32, "raw10", "tab_w1"))
-
-        def weave(engine_copy, g, a, woven=None):
-            woven = held([P, H, 4], BF16, "woven%d%d" % (g, a)) if woven is None else woven
-            engine_copy(
+        def weave(copy, g, a, woven):
+            copy(
                 woven[:].rearrange("p (c i) j -> p c j i", i=4),
                 raw[g, a][:].rearrange("p j (c i) -> p c j i", i=4),
             )
@@ -144,17 +121,8 @@ def tile_list_gated_pair_terms_kernel(
         def from_bank(bank):
             return bank[:].rearrange("t (p u e) -> t u p e", u=2, e=2)
 
-        def in_order(tile):
-            return tile.rearrange("t (u p e) -> t u p e", u=2, e=2)
-
-        h_cols = [held([P, HALF * 4], BF16, "h_cols%d" % h) for h in range(2)]
-        h_w = {}
-        h_s = [held([P, HALF], U8, "h_s%d" % h) for h in range(2)]
-        sig = {}
-        h_rows = {}
-
-        def bank_tile(b, shape):
-            return psum.tile(shape, F32, name="bank", tag="bank%d" % b)
+        def in_order(row):
+            return row.rearrange("t (u p e) -> t u p e", u=2, e=2)
 
         def gate(g, c, b, into):
             sig[g, c] = into
@@ -173,32 +141,31 @@ def tile_list_gated_pair_terms_kernel(
                 project(banks[ii], 2 * c + ii, lambda a: proj_w[g][a][:].bitcast(FP8X4), lambda a: proj_s[g][a][:])
             return banks
 
-        def pair(name, tag=None):
-            return held([P, 2, H], F32, name, tag)[:]
-
-        def times_left(left, factor, into):
+        def times_left(banks, factor, into):
             for ii in range(2):
-                nc.vector.tensor_tensor(in_order(into[:, ii, :]), from_bank(left[ii]), in_order(factor[:, ii, :]), MULT)
+                nc.vector.tensor_tensor(in_order(into[:, ii, :]), from_bank(banks[ii]), in_order(factor[:, ii, :]), MULT)
 
-        def times_right(c, right, factor):
+        def times_right(c, banks, factor):
             for ii in range(2):
                 h_rows[c, ii] = held([P, H], BF16, "h_rows%d%d" % (c, ii))
-                nc.vector.tensor_tensor(in_order(h_rows[c, ii][:]), from_bank(right[ii]), in_order(factor[ii]), MULT)
+                nc.vector.tensor_tensor(in_order(h_rows[c, ii][:]), from_bank(banks[ii]), in_order(factor[:, ii, :]), MULT)
 
         def turn(c, b):
             turned = bank_tile(b, [P, 4, P])
             for ii in range(2):
                 for u in range(2):
-                    nc.tensor.transpose(turned[:, 2 * ii + u, :], h_rows[c, ii][:].bitcast(F32)[:, P * u : P * (u + 1)], ident[:])
+                    words = h_rows[c, ii][:].bitcast(F32)[:, P * u : P * (u + 1)]
+                    nc.tensor.transpose(turned[:, 2 * ii + u, :], words, ident[:])
             h, cc = divmod(c, 2)
+            columns = h_cols[h][:].bitcast(F32)[:, cc * 2 * CHUNK : (cc + 1) * 2 * CHUNK]
             nc.scalar.copy(
-                h_cols[h][:].bitcast(F32)[:, cc * 2 * CHUNK : (cc + 1) * 2 * CHUNK].rearrange("p (i t u) -> p i t u", i=2, u=2),
+                columns.rearrange("p (i t u) -> p i t u", i=2, u=2),
                 turned[:].rearrange("p (i u) t -> p i t u", u=2),
             )
 
         def quantise_h(h, words):
             h_w[h] = words
-            nc.vector.quantize_mx(out=h_w[h][:].bitcast(FP8X4), scales=h_s[h][:], in_=h_cols[h][:])
+            nc.vector.quantize_mx(out=words[:].bitcast(FP8X4), scales=h_s[h][:], in_=h_cols[h][:])
 
         def out_project(h, n, y, b):
             bank = bank_tile(b, [P, HALF])
@@ -219,14 +186,47 @@ def tile_list_gated_pair_terms_kernel(
                 cache[n][:].indirect(entries(place, h)), y[:], wgo_sb[:, h * HALF : (h + 1) * HALF], MULT,
             )
 
+        nc.gpsimd.memset(tab_s[:].bitcast(I32), 0)
+
+        nc.sync.dma_start(pick[:], offs)
+        nc.sync.dma_start(place[:], offs2)
+        load_gate_scales(LEFT, (0,))
+        for q in range(4):
+            nc.sync.dma_start(
+                out=tab_s[:].bitcast(I32)[32 * q : 32 * q + 8, :],
+                in_=tab_scales.bitcast(I32)[:, 4 * q : 4 * q + 4, :],
+            )
+        load_table(0)
+        load_gate_scales(LEFT, (1, 2, 3))
+        load_gate_words(LEFT)
+        load_table(1)
+        load_gate_scales(RIGHT, range(4))
+
+        make_identity(nc, ident[:])
+        for n in range(ROW_TILES):
+            nc.gpsimd.memset(cache[n][:], 0.0)
+
+        nc.vector.tensor_copy(v_s[0][:], tab_s[:].indirect(pick[:]))
+        nc.sync.dma_start(out=v_s[1][:].bitcast(I32)[0:100, :], in_=v_s[0][:].bitcast(I32)[4:104, :])
+        load_raw(LEFT, 0, placed([P, 4, H], F32, "raw00", ABOVE))
+        gate_w[RIGHT] = placed([P, PASSES * 2 * H], U8, "gate_w1", BELOW)
+        load_gate_words(RIGHT)
+
+        for a in range(PASSES):
+            for h in range(2):
+                nc.vector.tensor_copy(v_w[h][a][:], tab_w[a][:].bitcast(U32).indirect(entries(pick, h)))
+
+        load_raw(LEFT, 1, held([P, 4, H], F32, "raw01", "tab_w0"))
+        load_raw(RIGHT, 0, held([P, 4, H], F32, "raw10", "tab_w1"))
+
         for c in range(4):
-            gate(0, c, 2 * c, pair("sig0%d" % c))
-        quantise_weight(0, 0, weave(nc.vector.tensor_copy, 0, 0))
-        load_raw(1, 1, placed([P, 4, H], F32, "raw11", 21568))
+            gate(LEFT, c, 2 * c, chunk_tile("sig0%d" % c))
+        quantise_weight(LEFT, 0, weave(nc.vector.tensor_copy, LEFT, 0, held([P, H, 4], BF16, "woven00")))
+        load_raw(RIGHT, 1, placed([P, 4, H], F32, "raw11", ABOVE))
         wo_w = held([P, N], I32, "wo_w", "woven00")
         nc.sync.dma_start(out=wo_w[:], in_=wo_words[0].rearrange("p c i -> p (c i)").bitcast(I32))
-        quantise_weight(0, 1, weave(nc.vector.tensor_copy, 0, 1))
-        wgo_sb = placed([P, S], F32, "wgo_sb", 5184)
+        quantise_weight(LEFT, 1, weave(nc.vector.tensor_copy, LEFT, 1, held([P, H, 4], BF16, "woven01")))
+        wgo_sb = held([P, S], F32, "wgo_sb", "tab_w0")
         nc.sync.dma_start(out=wgo_sb[:], in_=wgo)
         wo_s = held([P, N], U8, "wo_s", "woven01")
         for q in range(4):
@@ -235,50 +235,57 @@ def tile_list_gated_pair_terms_kernel(
                 in_=wo_scales[0].bitcast(I32)[4 * q : 4 * q + 4, :],
             )
         for c in range(2):
-            gate(1, c, 2 * c, pair("sig1%d" % c))
-        first_pass = weave(nc.vector.tensor_copy, 1, 0)
-        gates0 = pair("gates0", "tab_w1")
-        nc.vector.tensor_tensor(gates0, sig[0, 0], sig[1, 0], MULT)
-        quantise_weight(1, 0, first_pass)
-        second_pass = weave(nc.scalar.copy, 1, 1, held([P, H, 4], BF16, "woven11", "sig10"))
-        late_sigs = placed([P, 2, 2, H], F32, "late_sigs", 21568)
+            gate(RIGHT, c, 2 * c, chunk_tile("sig1%d" % c))
+
+        first_pass = weave(nc.vector.tensor_copy, RIGHT, 0, held([P, H, 4], BF16, "woven10"))
+        gates0 = chunk_tile("gates0", "tab_w1")
+        nc.vector.tensor_tensor(gates0, sig[LEFT, 0], sig[RIGHT, 0], MULT)
+        quantise_weight(RIGHT, 0, first_pass)
+
+        second_pass = weave(nc.scalar.copy, RIGHT, 1, held([P, H, 4], BF16, "woven11", "sig10"))
+        late_sigs = placed([P, 2, 2, H], F32, "late_sigs", ABOVE)
         for c in range(2, 4):
-            gate(1, c, 2 * c, late_sigs[:, c - 2])
-        gates1 = pair("gates1", "woven10")
-        nc.gpsimd.tensor_tensor(gates1, sig[0, 1], sig[1, 1], MULT)
-        left = {0: projection(0, 0, 0), 2: projection(0, 2, 2)}
-        twice = {c: pair("twice%d" % c) for c in (0, 1, 3)}
-        times_left(left[0], gates0, twice[0])
-        once2 = pair("once2", "sig00")
-        times_left(left[2], sig[0, 2], once2)
-        left[1] = projection(0, 1, 0)
-        quantise_weight(1, 1, second_pass)
-        later = held([P, 2, 2, H], F32, "later", "sig10")
-        twice[2] = later[:, 0]
-        gates3 = later[:, 1]
-        nc.gpsimd.tensor_tensor(twice[2], once2, sig[1, 2], MULT)
-        nc.gpsimd.tensor_tensor(gates3, sig[0, 3], sig[1, 3], MULT)
-        right = [projection(1, c, 2 + 2 * c) for c in range(3)]
-        times_left(left[1], gates1, twice[1])
-        times_right(0, right[0], (twice[0][:, 0], twice[0][:, 1]))
+            gate(RIGHT, c, 2 * c, late_sigs[:, c - 2])
+
+        gates1 = chunk_tile("gates1", "woven10")
+        nc.gpsimd.tensor_tensor(gates1, sig[LEFT, 1], sig[RIGHT, 1], MULT)
+        left = {0: projection(LEFT, 0, 0), 2: projection(LEFT, 2, 2)}
+        gated = {c: chunk_tile("gated%d" % c) for c in (0, 1, 3)}
+        times_left(left[0], gates0, gated[0])
+        half_gated2 = chunk_tile("half_gated2", "sig00")
+        times_left(left[2], sig[LEFT, 2], half_gated2)
+        left[1] = projection(LEFT, 1, 0)
+        quantise_weight(RIGHT, 1, second_pass)
+        after_weights = held([P, 2, 2, H], F32, "after_weights", "sig10")
+        gated[2] = after_weights[:, 0]
+        gates3 = after_weights[:, 1]
+        nc.gpsimd.tensor_tensor(gated[2], half_gated2, sig[RIGHT, 2], MULT)
+        nc.gpsimd.tensor_tensor(gates3, sig[LEFT, 3], sig[RIGHT, 3], MULT)
+
+        right = [projection(RIGHT, c, 2 + 2 * c) for c in range(3)]
+        times_left(left[1], gates1, gated[1])
+        times_right(0, right[0], gated[0])
         turn(0, 2)
-        times_right(1, right[1], (twice[1][:, 0], twice[1][:, 1]))
+        times_right(1, right[1], gated[1])
         turn(1, 4)
-        left[3] = projection(0, 3, 0)
-        times_right(2, right[2], (twice[2][:, 0], twice[2][:, 1]))
-        quantise_h(0, placed([P, HALF], U32, "h_w0", 21568))
+        left[3] = projection(LEFT, 3, 0)
+        times_right(2, right[2], gated[2])
+
+        quantise_h(0, placed([P, HALF], U32, "h_w0", ABOVE))
         y_first = out_project(0, 0, held([P, HALF], F32, "y00"), 3)
-        right.append(projection(1, 3, 6))
-        times_left(left[3], gates3, twice[3])
+        right.append(projection(RIGHT, 3, 6))
+        times_left(left[3], gates3, gated[3])
         turn(2, 5)
-        times_right(3, right[3], (twice[3][:, 0], twice[3][:, 1]))
+        times_right(3, right[3], gated[3])
         turn(3, 0)
+
         scatter(0, 0, y_first)
         quantise_h(1, held([P, HALF], U32, "h_w1"))
         scatter(0, 1, out_project(0, 1, held([P, HALF], F32, "y01", "h_rows31"), 1))
         scatter(0, 2, out_project(0, 2, held([P, HALF], F32, "y02", "h_cols1"), 2))
         for n in range(ROW_TILES):
             scatter(1, n, out_project(1, n, held([P, HALF], F32, "y1%d" % n), 3 + n))
+
         for n in range(ROW_TILES):
             for queue, cols in ((nc.sync, slice(0, T2 // 2)), (nc.scalar, slice(T2 // 2, T2))):
                 queue.dma_start(out=out[n * P : (n + 1) * P, cols], in_=cache[n][:, cols])

@@ -55,7 +55,7 @@ def tile_list_gated_pair_terms_kernel(
 
         tab_w = [held([P, T], I32, "tab_w%d" % a) for a in range(PASSES)]
         tab_s = placed([P, T], U8, "tab_s", TABLE_SCALES)
-        v_w = [[held([P, HALF], U32, "v_w%d%d" % (h, a)) for a in range(PASSES)] for h in range(2)]
+        v_w = [[held([P, HALF], U32, "v_w%d%d" % (half, a)) for a in range(PASSES)] for half in range(2)]
         v_s = [held([P, S], U8, "v_s%d" % a) for a in range(PASSES)]
         gate_w = {LEFT: held([P, PASSES * 2 * H], U8, "gate_w0")}
         gate_s = [held([P, PASSES * H], U8, "gate_s%d" % g) for g in range(2)]
@@ -63,8 +63,8 @@ def tile_list_gated_pair_terms_kernel(
         proj_s = [[held([P, H], U8, "proj_s%d%d" % (g, a)) for a in range(PASSES)] for g in range(2)]
         cache = [held([P, T2], F32, "cache%d" % n) for n in range(ROW_TILES)]
         ident = held([P, P], F32, "ident")
-        h_cols = [held([P, HALF * 4], BF16, "h_cols%d" % h) for h in range(2)]
-        h_s = [held([P, HALF], U8, "h_s%d" % h) for h in range(2)]
+        h_cols = [held([P, HALF * 4], BF16, "h_cols%d" % half) for half in range(2)]
+        h_s = [held([P, HALF], U8, "h_s%d" % half) for half in range(2)]
         raw, sig, h_rows, h_w = {}, {}, {}, {}
 
         def load_raw(g, a, tile):
@@ -85,11 +85,11 @@ def tile_list_gated_pair_terms_kernel(
             for q in quadrants:
                 nc.sync.dma_start(
                     out=gate_s[g][:].bitcast(I32)[32 * q : 32 * q + 4, :],
-                    in_=(gl_scales, gr_scales)[g].bitcast(I32)[:, 4 * q : 4 * q + 4, :].rearrange("a r c -> r a c"),
+                    in_=(gl_scales, gr_scales)[g].bitcast(I32)[:, 4 * q : 4 * q + 4, :].rearrange("a m c -> m a c"),
                 )
 
-        def entries(offsets, h):
-            return offsets[:, h * (HALF // 16) : (h + 1) * (HALF // 16)]
+        def entries(offsets, half):
+            return offsets[:, half * (HALF // 16) : (half + 1) * (HALF // 16)]
 
         def weave(copy, g, a, woven):
             copy(
@@ -106,11 +106,11 @@ def tile_list_gated_pair_terms_kernel(
             )
 
         def project(bank, i, words, scales):
-            h, j = divmod(i * P, HALF)
+            half, j = divmod(i * P, HALF)
             for a in range(PASSES):
                 nc.tensor.matmul_mx(
                     out=bank[:],
-                    lhsT=v_w[h][a][:, j : j + P].bitcast(FP8X4),
+                    lhsT=v_w[half][a][:, j : j + P].bitcast(FP8X4),
                     lhsT_scale=v_s[a][:, i * P : (i + 1) * P],
                     rhs=words(a),
                     rhs_scale=scales(a),
@@ -126,64 +126,64 @@ def tile_list_gated_pair_terms_kernel(
 
         def gate(g, c, b, into):
             sig[g, c] = into
-            for ii in range(2):
-                bank = bank_tile(b + ii, [P, H])
+            for sub in range(2):
+                bank = bank_tile(b + sub, [P, H])
                 project(
-                    bank, 2 * c + ii,
+                    bank, 2 * c + sub,
                     lambda a: gate_w[g][:, 2 * H * a : 2 * H * (a + 1)].bitcast(FP4X4),
                     lambda a: gate_s[g][:, H * a : H * (a + 1)],
                 )
-                nc.scalar.activation(in_order(into[:, ii, :]), from_bank(bank), SIGMOID)
+                nc.scalar.activation(in_order(into[:, sub, :]), from_bank(bank), SIGMOID)
 
         def projection(g, c, b):
-            banks = [bank_tile(b + ii, [P, H]) for ii in range(2)]
-            for ii in range(2):
-                project(banks[ii], 2 * c + ii, lambda a: proj_w[g][a][:].bitcast(FP8X4), lambda a: proj_s[g][a][:])
+            banks = [bank_tile(b + sub, [P, H]) for sub in range(2)]
+            for sub in range(2):
+                project(banks[sub], 2 * c + sub, lambda a: proj_w[g][a][:].bitcast(FP8X4), lambda a: proj_s[g][a][:])
             return banks
 
         def times_left(banks, factor, into):
-            for ii in range(2):
-                nc.vector.tensor_tensor(in_order(into[:, ii, :]), from_bank(banks[ii]), in_order(factor[:, ii, :]), MULT)
+            for sub in range(2):
+                nc.vector.tensor_tensor(in_order(into[:, sub, :]), from_bank(banks[sub]), in_order(factor[:, sub, :]), MULT)
 
         def times_right(c, banks, factor):
-            for ii in range(2):
-                h_rows[c, ii] = held([P, H], BF16, "h_rows%d%d" % (c, ii))
-                nc.vector.tensor_tensor(in_order(h_rows[c, ii][:]), from_bank(banks[ii]), in_order(factor[:, ii, :]), MULT)
+            for sub in range(2):
+                h_rows[c, sub] = held([P, H], BF16, "h_rows%d%d" % (c, sub))
+                nc.vector.tensor_tensor(in_order(h_rows[c, sub][:]), from_bank(banks[sub]), in_order(factor[:, sub, :]), MULT)
 
         def turn(c, b):
             turned = bank_tile(b, [P, 4, P])
-            for ii in range(2):
+            for sub in range(2):
                 for u in range(2):
-                    words = h_rows[c, ii][:].bitcast(F32)[:, P * u : P * (u + 1)]
-                    nc.tensor.transpose(turned[:, 2 * ii + u, :], words, ident[:])
-            h, cc = divmod(c, 2)
-            columns = h_cols[h][:].bitcast(F32)[:, cc * 2 * CHUNK : (cc + 1) * 2 * CHUNK]
+                    words = h_rows[c, sub][:].bitcast(F32)[:, P * u : P * (u + 1)]
+                    nc.tensor.transpose(turned[:, 2 * sub + u, :], words, ident[:])
+            half, c_in_half = divmod(c, 2)
+            columns = h_cols[half][:].bitcast(F32)[:, c_in_half * 2 * CHUNK : (c_in_half + 1) * 2 * CHUNK]
             nc.scalar.copy(
                 columns.rearrange("p (i t u) -> p i t u", i=2, u=2),
                 turned[:].rearrange("p (i u) t -> p i t u", u=2),
             )
 
-        def quantise_h(h, words):
-            h_w[h] = words
-            nc.vector.quantize_mx(out=words[:].bitcast(FP8X4), scales=h_s[h][:], in_=h_cols[h][:])
+        def quantise_h(half, words):
+            h_w[half] = words
+            nc.vector.quantize_mx(out=words[:].bitcast(FP8X4), scales=h_s[half][:], in_=h_cols[half][:])
 
-        def out_project(h, n, y, b):
+        def out_project(half, n, y, b):
             bank = bank_tile(b, [P, HALF])
             nc.tensor.matmul_mx(
                 out=bank[:],
                 lhsT=wo_w[:, n * P : (n + 1) * P].bitcast(FP8X4),
                 lhsT_scale=wo_s[:, n * P : (n + 1) * P],
-                rhs=h_w[h][:].bitcast(FP8X4),
-                rhs_scale=h_s[h][:],
+                rhs=h_w[half][:].bitcast(FP8X4),
+                rhs_scale=h_s[half][:],
                 start=True,
                 stop=True,
             )
             nc.scalar.copy(y[:], bank[:])
             return y
 
-        def scatter(h, n, y):
+        def scatter(half, n, y):
             nc.vector.tensor_tensor(
-                cache[n][:].indirect(entries(place, h)), y[:], wgo_sb[:, h * HALF : (h + 1) * HALF], MULT,
+                cache[n][:].indirect(entries(place, half)), y[:], wgo_sb[:, half * HALF : (half + 1) * HALF], MULT,
             )
 
         nc.gpsimd.memset(tab_s[:].bitcast(I32), 0)
@@ -213,8 +213,8 @@ def tile_list_gated_pair_terms_kernel(
         load_gate_words(RIGHT)
 
         for a in range(PASSES):
-            for h in range(2):
-                nc.vector.tensor_copy(v_w[h][a][:], tab_w[a][:].bitcast(U32).indirect(entries(pick, h)))
+            for half in range(2):
+                nc.vector.tensor_copy(v_w[half][a][:], tab_w[a][:].bitcast(U32).indirect(entries(pick, half)))
 
         load_raw(LEFT, 1, held([P, 4, H], F32, "raw01", "tab_w0"))
         load_raw(RIGHT, 0, held([P, 4, H], F32, "raw10", "tab_w1"))
@@ -287,5 +287,4 @@ def tile_list_gated_pair_terms_kernel(
             scatter(1, n, out_project(1, n, held([P, HALF], F32, "y1%d" % n), 3 + n))
 
         for n in range(ROW_TILES):
-            for queue, cols in ((nc.sync, slice(0, T2 // 2)), (nc.scalar, slice(T2 // 2, T2))):
-                queue.dma_start(out=out[n * P : (n + 1) * P, cols], in_=cache[n][:, cols])
+            nc.sync.dma_start(out=out[n * P : (n + 1) * P, :], in_=cache[n][:])

@@ -24,7 +24,19 @@ CHUNK = 256
 ROW_TILES = N // P
 LEFT, RIGHT = 0, 1
 
-BELOW, TABLE_SCALES, ABOVE = 0, T // 2, T
+TILES = S // P
+KIB = 1024
+
+AT_WL = (8 * KIB, 0)
+AT_TABLE_SCALES = 7 * KIB
+AT_TABLE = (16 * KIB, 34 * KIB)
+AT_RIGHT_GATE = 17 * KIB
+AT_WR = (19 * KIB, 27 * KIB)
+AT_WO_WORDS, AT_WO_SCALES, AT_WGO = 36 * KIB, 37 * KIB + 512, 38 * KIB
+AT_LATE_SIGS = 26 * KIB
+AT_LAST_WOVEN = 42 * KIB
+EARLY_SIGS = 3
+PIECES = ((0, 256), (256, 256), (512, 512))
 
 
 def tile_list_gated_pair_terms_kernel(
@@ -47,30 +59,29 @@ def tile_list_gated_pair_terms_kernel(
         def bank_tile(b, shape):
             return psum.tile(shape, F32, name="bank", tag="bank%d" % b)
 
-        def chunk_tile(name, on=None):
-            return held([P, 2, H], F32, name, on)[:]
+        def late_sig_bytes(shape, dtype, name, i):
+            return placed(shape, dtype, name, AT_LATE_SIGS + 2 * KIB * (i - EARLY_SIGS))
 
         pick = lists.tile([P, S // 16], U16, name="pick")
         place = lists.tile([P, S // 16], U16, name="place")
 
-        tab_w = [held([P, T], I32, "tab_w%d" % a) for a in range(PASSES)]
-        tab_s = placed([P, T], U8, "tab_s", TABLE_SCALES)
-        v_w = [[held([P, HALF], U32, "v_w%d%d" % (half, a)) for a in range(PASSES)] for half in range(2)]
+        tab_w = [placed([P, T], I32, "tab_w%d" % a, AT_TABLE[a]) for a in range(PASSES)]
+        tab_s = placed([P, T], U8, "tab_s", AT_TABLE_SCALES)
+        v_w = {}
         v_s = [held([P, S], U8, "v_s%d" % a) for a in range(PASSES)]
         gate_w = {LEFT: held([P, PASSES * 2 * H], U8, "gate_w0")}
         gate_s = [held([P, PASSES * H], U8, "gate_s%d" % g) for g in range(2)]
-        proj_w = [[held([P, H], U32, "proj_w%d%d" % (g, a)) for a in range(PASSES)] for g in range(2)]
         proj_s = [[held([P, H], U8, "proj_s%d%d" % (g, a)) for a in range(PASSES)] for g in range(2)]
         cache = [held([P, T2], F32, "cache%d" % n) for n in range(ROW_TILES)]
         ident = held([P, P], F32, "ident")
         h_cols = [held([P, HALF * 4], BF16, "h_cols%d" % half) for half in range(2)]
         h_s = [held([P, HALF], U8, "h_s%d" % half) for half in range(2)]
-        raw, sig, h_rows, h_w = {}, {}, {}, {}
+        raw, woven, proj_w, banks, sig, gated, h_rows, h_w = {}, {}, {}, {}, {}, {}, {}, {}
 
-        def load_raw(g, a, tile):
-            raw[g, a] = tile
+        def load_raw(g, a):
+            raw[g, a] = placed([P, 4, H], F32, "raw%d%d" % (g, a), (AT_WL, AT_WR)[g][a])
             rows = (wl, wr)[g][512 * a : 512 * (a + 1), :]
-            nc.sync.dma_start(out=tile[:], in_=rows.rearrange("(p j) c -> p j c", j=4))
+            nc.sync.dma_start(out=raw[g, a][:], in_=rows.rearrange("(p j) c -> p j c", j=4))
 
         def load_table(a):
             nc.sync.dma_start(out=tab_w[a][:], in_=tab_words[a].rearrange("p t i -> p (t i)").bitcast(I32))
@@ -88,78 +99,89 @@ def tile_list_gated_pair_terms_kernel(
                     in_=(gl_scales, gr_scales)[g].bitcast(I32)[:, 4 * q : 4 * q + 4, :].rearrange("a m c -> m a c"),
                 )
 
-        def entries(offsets, half):
-            return offsets[:, half * (HALF // 16) : (half + 1) * (HALF // 16)]
+        def entries(offsets, first, count):
+            return offsets[:, first // 16 : (first + count) // 16]
 
-        def weave(copy, g, a, woven):
+        def gather_words(a):
+            for first, count in PIECES:
+                piece = held([P, count], U32, "v_w%d_%d" % (a, first))
+                nc.vector.tensor_copy(piece[:], tab_w[a][:].bitcast(U32).indirect(entries(pick, first, count)))
+                for j in range(0, count, P):
+                    v_w[a, (first + j) // P] = piece[:, j : j + P]
+
+        def weave(copy, g, a, into=None):
+            woven[g, a] = into or held([P, H, 4], BF16, "woven%d%d" % (g, a))
             copy(
-                woven[:].rearrange("p (c i) j -> p c j i", i=4),
+                woven[g, a][:].rearrange("p (c i) j -> p c j i", i=4),
                 raw[g, a][:].rearrange("p j (c i) -> p c j i", i=4),
             )
-            return woven
 
-        def quantise_weight(g, a, woven):
+        def quantise_weight(g, a, on=None):
+            proj_w[g, a] = held([P, H], U32, "proj_w%d%d" % (g, a), on)
             nc.vector.quantize_mx(
-                out=proj_w[g][a][:].bitcast(FP8X4),
+                out=proj_w[g, a][:].bitcast(FP8X4),
                 scales=proj_s[g][a][:],
-                in_=woven[:].rearrange("p c j -> p (c j)"),
+                in_=woven[g, a][:].rearrange("p c j -> p (c j)"),
             )
 
-        def project(bank, i, words, scales):
-            half, j = divmod(i * P, HALF)
+        def project(b, i, words, scales):
+            bank = bank_tile(b, [P, H])
             for a in range(PASSES):
                 nc.tensor.matmul_mx(
                     out=bank[:],
-                    lhsT=v_w[half][a][:, j : j + P].bitcast(FP8X4),
+                    lhsT=v_w[a, i].bitcast(FP8X4),
                     lhsT_scale=v_s[a][:, i * P : (i + 1) * P],
                     rhs=words(a),
                     rhs_scale=scales(a),
                     start=(a == 0),
                     stop=(a == PASSES - 1),
                 )
+            return bank
 
         def from_bank(bank):
             return bank[:].rearrange("t (p u e) -> t u p e", u=2, e=2)
 
         def in_order(row):
-            return row.rearrange("t (u p e) -> t u p e", u=2, e=2)
+            return row[:].rearrange("t (u p e) -> t u p e", u=2, e=2)
 
-        def gate(g, c, b, into):
-            sig[g, c] = into
-            for sub in range(2):
-                bank = bank_tile(b + sub, [P, H])
-                project(
-                    bank, 2 * c + sub,
-                    lambda a: gate_w[g][:, 2 * H * a : 2 * H * (a + 1)].bitcast(FP4X4),
-                    lambda a: gate_s[g][:, H * a : H * (a + 1)],
-                )
-                nc.scalar.activation(in_order(into[:, sub, :]), from_bank(bank), SIGMOID)
+        def gate(g, i, b, into):
+            sig[g, i] = into
+            bank = project(
+                b, i,
+                lambda a: gate_w[g][:, 2 * H * a : 2 * H * (a + 1)].bitcast(FP4X4),
+                lambda a: gate_s[g][:, H * a : H * (a + 1)],
+            )
+            nc.scalar.activation(in_order(into), from_bank(bank), SIGMOID)
 
-        def projection(g, c, b):
-            banks = [bank_tile(b + sub, [P, H]) for sub in range(2)]
-            for sub in range(2):
-                project(banks[sub], 2 * c + sub, lambda a: proj_w[g][a][:].bitcast(FP8X4), lambda a: proj_s[g][a][:])
-            return banks
+        def late_gate(i, b):
+            gate(RIGHT, i, b, late_sig_bytes([P, H], F32, "sig1%d" % i, i))
 
-        def times_left(banks, factor, into):
-            for sub in range(2):
-                nc.vector.tensor_tensor(in_order(into[:, sub, :]), from_bank(banks[sub]), in_order(factor[:, sub, :]), MULT)
+        def projection(g, i, b):
+            banks[g, i] = project(b, i, lambda a: proj_w[g, a][:].bitcast(FP8X4), lambda a: proj_s[g][a][:])
 
-        def times_right(c, banks, factor):
-            for sub in range(2):
-                h_rows[c, sub] = held([P, H], BF16, "h_rows%d%d" % (c, sub))
-                nc.vector.tensor_tensor(in_order(h_rows[c, sub][:]), from_bank(banks[sub]), in_order(factor[:, sub, :]), MULT)
+        def times_left(i, into=None):
+            gated[i] = into or held([P, H], F32, "gated%d" % i)
+            nc.vector.tensor_tensor(in_order(gated[i]), from_bank(banks[LEFT, i]), in_order(sig[LEFT, i]), MULT)
 
-        def turn(c, b):
-            turned = bank_tile(b, [P, 4, P])
-            for sub in range(2):
+        def times_right_gate(engine, i, into=None):
+            source = gated[i]
+            gated[i] = into or source
+            engine.tensor_tensor(gated[i][:], source[:], sig[RIGHT, i][:], MULT)
+
+        def times_right(i):
+            h_rows[i] = held([P, H], BF16, "h_rows%d" % i)
+            nc.vector.tensor_tensor(in_order(h_rows[i]), from_bank(banks[RIGHT, i]), in_order(gated[i]), MULT)
+
+        def turn(tiles, b):
+            turned = bank_tile(b, [P, 2 * len(tiles), P])
+            for sub, i in enumerate(tiles):
                 for u in range(2):
-                    words = h_rows[c, sub][:].bitcast(F32)[:, P * u : P * (u + 1)]
+                    words = h_rows[i][:].bitcast(F32)[:, P * u : P * (u + 1)]
                     nc.tensor.transpose(turned[:, 2 * sub + u, :], words, ident[:])
-            half, c_in_half = divmod(c, 2)
-            columns = h_cols[half][:].bitcast(F32)[:, c_in_half * 2 * CHUNK : (c_in_half + 1) * 2 * CHUNK]
+            half, first = divmod(tiles[0], TILES // 2)
+            columns = h_cols[half][:].bitcast(F32)[:, 2 * P * first : 2 * P * (first + len(tiles))]
             nc.scalar.copy(
-                columns.rearrange("p (i t u) -> p i t u", i=2, u=2),
+                columns.rearrange("p (i t u) -> p i t u", i=len(tiles), u=2),
                 turned[:].rearrange("p (i u) t -> p i t u", u=2),
             )
 
@@ -167,7 +189,7 @@ def tile_list_gated_pair_terms_kernel(
             h_w[half] = words
             nc.vector.quantize_mx(out=words[:].bitcast(FP8X4), scales=h_s[half][:], in_=h_cols[half][:])
 
-        def out_project(half, n, y, b):
+        def out_matmul(half, n, b):
             bank = bank_tile(b, [P, HALF])
             nc.tensor.matmul_mx(
                 out=bank[:],
@@ -178,12 +200,16 @@ def tile_list_gated_pair_terms_kernel(
                 start=True,
                 stop=True,
             )
-            nc.scalar.copy(y[:], bank[:])
+            return bank
+
+        def out_project(half, n, y, b):
+            nc.scalar.copy(y[:], out_matmul(half, n, b)[:])
             return y
 
         def scatter(half, n, y):
             nc.vector.tensor_tensor(
-                cache[n][:].indirect(entries(place, half)), y[:], wgo_sb[:, half * HALF : (half + 1) * HALF], MULT,
+                cache[n][:].indirect(entries(place, half * HALF, HALF)), y[:],
+                wgo_sb[:, half * HALF : (half + 1) * HALF], MULT,
             )
 
         nc.gpsimd.memset(tab_s[:].bitcast(I32), 0)
@@ -208,81 +234,95 @@ def tile_list_gated_pair_terms_kernel(
 
         nc.vector.tensor_copy(v_s[0][:], tab_s[:].indirect(pick[:]))
         nc.sync.dma_start(out=v_s[1][:].bitcast(I32)[0:100, :], in_=v_s[0][:].bitcast(I32)[4:104, :])
-        load_raw(LEFT, 0, placed([P, 4, H], F32, "raw00", ABOVE))
-        gate_w[RIGHT] = placed([P, PASSES * 2 * H], U8, "gate_w1", BELOW)
+        load_raw(LEFT, 0)
+        load_raw(LEFT, 1)
+
+        gather_words(0)
+        gate_w[RIGHT] = placed([P, PASSES * 2 * H], U8, "gate_w1", AT_RIGHT_GATE)
         load_gate_words(RIGHT)
-
-        for a in range(PASSES):
-            for half in range(2):
-                nc.vector.tensor_copy(v_w[half][a][:], tab_w[a][:].bitcast(U32).indirect(entries(pick, half)))
-
-        load_raw(LEFT, 1, held([P, 4, H], F32, "raw01", "tab_w0"))
-        load_raw(RIGHT, 0, held([P, 4, H], F32, "raw10", "tab_w1"))
-
-        for c in range(4):
-            gate(LEFT, c, 2 * c, chunk_tile("sig0%d" % c))
-        quantise_weight(LEFT, 0, weave(nc.vector.tensor_copy, LEFT, 0, held([P, H, 4], BF16, "woven00")))
-        load_raw(RIGHT, 1, placed([P, 4, H], F32, "raw11", ABOVE))
-        wo_w = held([P, N], I32, "wo_w", "woven00")
+        load_raw(RIGHT, 0)
+        gather_words(1)
+        load_raw(RIGHT, 1)
+        wo_w = placed([P, N], I32, "wo_w", AT_WO_WORDS)
         nc.sync.dma_start(out=wo_w[:], in_=wo_words[0].rearrange("p c i -> p (c i)").bitcast(I32))
-        quantise_weight(LEFT, 1, weave(nc.vector.tensor_copy, LEFT, 1, held([P, H, 4], BF16, "woven01")))
-        wgo_sb = held([P, S], F32, "wgo_sb", "tab_w0")
-        nc.sync.dma_start(out=wgo_sb[:], in_=wgo)
-        wo_s = held([P, N], U8, "wo_s", "woven01")
+        wo_s = placed([P, N], U8, "wo_s", AT_WO_SCALES)
         for q in range(4):
             nc.sync.dma_start(
                 out=wo_s[:].bitcast(I32)[32 * q : 32 * q + 4, :],
                 in_=wo_scales[0].bitcast(I32)[4 * q : 4 * q + 4, :],
             )
-        for c in range(2):
-            gate(RIGHT, c, 2 * c, chunk_tile("sig1%d" % c))
+        wgo_sb = placed([P, S], F32, "wgo_sb", AT_WGO)
+        nc.sync.dma_start(out=wgo_sb[:], in_=wgo)
 
-        first_pass = weave(nc.vector.tensor_copy, RIGHT, 0, held([P, H, 4], BF16, "woven10"))
-        gates0 = chunk_tile("gates0", "tab_w1")
-        nc.vector.tensor_tensor(gates0, sig[LEFT, 0], sig[RIGHT, 0], MULT)
-        quantise_weight(RIGHT, 0, first_pass)
+        for i in range(TILES):
+            gate(LEFT, i, i, held([P, H], F32, "sig0%d" % i))
+        for a in range(PASSES):
+            weave(nc.vector.tensor_copy, LEFT, a)
+            quantise_weight(LEFT, a)
 
-        second_pass = weave(nc.scalar.copy, RIGHT, 1, held([P, H, 4], BF16, "woven11", "sig10"))
-        late_sigs = placed([P, 2, 2, H], F32, "late_sigs", ABOVE)
-        for c in range(2, 4):
-            gate(RIGHT, c, 2 * c, late_sigs[:, c - 2])
+        for i in range(2):
+            projection(LEFT, i, 3 + i)
+        for b, i in enumerate((2, 0, 1)):
+            gate(RIGHT, i, b, held([P, H], F32, "sig1%d" % i))
+        for i in range(2, 5):
+            projection(LEFT, i, i - 2)
+        weave(nc.scalar.copy, RIGHT, 0)
+        weave(nc.scalar.copy, RIGHT, 1, placed([P, H, 4], BF16, "woven11", AT_LAST_WOVEN))
+        both_gates = held([P, H], F32, "both_gates", "woven01")
+        nc.gpsimd.tensor_tensor(both_gates[:], sig[LEFT, 2][:], sig[RIGHT, 2][:], MULT)
+        sig[LEFT, 2] = both_gates
+        for i in range(3):
+            times_left(i)
+            projection(LEFT, 5 + i, (3 + i) % 5)
+            if i < 2:
+                times_right_gate(nc.gpsimd, i)
+        for i in range(3, 6):
+            times_left(i)
+            late_gate(i, i - 2)
+        times_left(6)
+        quantise_weight(RIGHT, 0, "sig11")
+        quantise_weight(RIGHT, 1)
+        for i in range(3):
+            projection(RIGHT, i, 5 + i)
+        times_left(7, placed([P, H], F32, "gated7", AT_LAST_WOVEN + 2 * KIB))
+        times_right_gate(nc.gpsimd, 3, placed([P, H], F32, "gated3_both", AT_LAST_WOVEN))
+        for i in range(3, 5):
+            projection(RIGHT, i, i - 3)
+        times_right_gate(nc.gpsimd, 4)
+        times_right_gate(nc.gpsimd, 5)
 
-        gates1 = chunk_tile("gates1", "woven10")
-        nc.gpsimd.tensor_tensor(gates1, sig[LEFT, 1], sig[RIGHT, 1], MULT)
-        left = {0: projection(LEFT, 0, 0), 2: projection(LEFT, 2, 2)}
-        gated = {c: chunk_tile("gated%d" % c) for c in (0, 1, 3)}
-        times_left(left[0], gates0, gated[0])
-        half_gated2 = chunk_tile("half_gated2", "sig00")
-        times_left(left[2], sig[LEFT, 2], half_gated2)
-        left[1] = projection(LEFT, 1, 0)
-        quantise_weight(RIGHT, 1, second_pass)
-        after_weights = held([P, 2, 2, H], F32, "after_weights", "sig10")
-        gated[2] = after_weights[:, 0]
-        gates3 = after_weights[:, 1]
-        nc.gpsimd.tensor_tensor(gated[2], half_gated2, sig[RIGHT, 2], MULT)
-        nc.gpsimd.tensor_tensor(gates3, sig[LEFT, 3], sig[RIGHT, 3], MULT)
+        times_right(0)
+        times_right(1)
+        turn((0, 1), 5)
+        times_right(2)
+        turn((2,), 6)
+        times_right(3)
+        turn((3,), 7)
+        projection(RIGHT, 5, 2)
+        late_gate(6, 5)
+        times_right(4)
+        quantise_h(0, late_sig_bytes([P, HALF], U32, "h_w0", 5))
+        y_bank = out_matmul(0, 0, 0)
+        times_right(5)
+        late_gate(7, 6)
+        projection(RIGHT, 7, 1)
+        projection(RIGHT, 6, 2)
+        times_right_gate(nc.gpsimd, 6, held([P, H], F32, "gated6_both", "h_cols0"))
+        times_right_gate(nc.gpsimd, 7)
+        y_first = held([P, HALF], F32, "y00")
+        nc.vector.tensor_tensor(y_first[:], y_bank[:], wgo_sb[:, :HALF], MULT)
+        nc.vector.tensor_copy(cache[0][:].indirect(entries(place, 0, HALF)), y_first[:])
+        turn((4, 5), 3)
+        right7 = held([P, H], F32, "right7")
+        nc.scalar.copy(in_order(right7), from_bank(banks[RIGHT, 7]))
+        h_rows[7] = held([P, H], BF16, "h_rows7")
+        nc.gpsimd.tensor_tensor(h_rows[7][:], right7[:], gated[7][:], MULT)
+        times_right(6)
+        turn((6, 7), 4)
 
-        right = [projection(RIGHT, c, 2 + 2 * c) for c in range(3)]
-        times_left(left[1], gates1, gated[1])
-        times_right(0, right[0], gated[0])
-        turn(0, 2)
-        times_right(1, right[1], gated[1])
-        turn(1, 4)
-        left[3] = projection(LEFT, 3, 0)
-        times_right(2, right[2], gated[2])
-
-        quantise_h(0, placed([P, HALF], U32, "h_w0", ABOVE))
-        y_first = out_project(0, 0, held([P, HALF], F32, "y00"), 3)
-        right.append(projection(RIGHT, 3, 6))
-        times_left(left[3], gates3, gated[3])
-        turn(2, 5)
-        times_right(3, right[3], gated[3])
-        turn(3, 0)
-
-        scatter(0, 0, y_first)
+        scatter(0, 1, out_project(0, 1, held([P, HALF], F32, "y01", "gated6"), 7))
         quantise_h(1, held([P, HALF], U32, "h_w1"))
-        scatter(0, 1, out_project(0, 1, held([P, HALF], F32, "y01", "h_rows31"), 1))
-        scatter(0, 2, out_project(0, 2, held([P, HALF], F32, "y02", "h_cols1"), 2))
+        scatter(0, 2, out_project(0, 2, held([P, HALF], F32, "y02", "h_rows7"), 0))
         for n in range(ROW_TILES):
             scatter(1, n, out_project(1, n, held([P, HALF], F32, "y1%d" % n), 3 + n))
 

@@ -35,6 +35,7 @@ AT_WR = (19 * KIB, 27 * KIB)
 AT_WO_WORDS, AT_WO_SCALES, AT_WGO = 36 * KIB, 37 * KIB + 512, 38 * KIB
 AT_LATE_SIGS = 26 * KIB
 AT_LAST_WOVEN = 42 * KIB
+GROUPS = (((0, 1),), ((2, 3), (4,)), ((5, 6), (7,)))
 EARLY_SIGS = 3
 PIECES = ((0, 256), (256, 256), (512, 512))
 
@@ -74,9 +75,8 @@ def tile_list_gated_pair_terms_kernel(
         proj_s = [[held([P, H], U8, "proj_s%d%d" % (g, a)) for a in range(PASSES)] for g in range(2)]
         cache = [held([P, T2], F32, "cache%d" % n) for n in range(ROW_TILES)]
         ident = held([P, P], F32, "ident")
-        h_cols = [held([P, HALF * 4], BF16, "h_cols%d" % half) for half in range(2)]
-        h_s = [held([P, HALF], U8, "h_s%d" % half) for half in range(2)]
-        raw, woven, proj_w, banks, sig, gated, h_rows, h_w = {}, {}, {}, {}, {}, {}, {}, {}
+        raw, woven, proj_w, banks, sig, gated, h_rows = {}, {}, {}, {}, {}, {}, {}
+        h_cols, h_w, h_s = {}, {}, {}
 
         def load_raw(g, a):
             raw[g, a] = placed([P, 4, H], F32, "raw%d%d" % (g, a), (AT_WL, AT_WR)[g][a])
@@ -168,8 +168,8 @@ def tile_list_gated_pair_terms_kernel(
             gated[i] = into or source
             engine.tensor_tensor(gated[i][:], source[:], sig[RIGHT, i][:], MULT)
 
-        def times_right(i):
-            h_rows[i] = held([P, H], BF16, "h_rows%d" % i)
+        def times_right(i, into=None):
+            h_rows[i] = into or held([P, H], BF16, "h_rows%d" % i)
             nc.vector.tensor_tensor(in_order(h_rows[i]), from_bank(banks[RIGHT, i]), in_order(gated[i]), MULT)
 
         def turn(tiles, b):
@@ -178,62 +178,103 @@ def tile_list_gated_pair_terms_kernel(
                 for u in range(2):
                     words = h_rows[i][:].bitcast(F32)[:, P * u : P * (u + 1)]
                     nc.tensor.transpose(turned[:, 2 * sub + u, :], words, ident[:])
-            half, first = divmod(tiles[0], TILES // 2)
-            columns = h_cols[half][:].bitcast(F32)[:, 2 * P * first : 2 * P * (first + len(tiles))]
+            h_cols[tiles] = held([P, 4 * P * len(tiles)], BF16, "h_cols%d" % tiles[0])
             nc.scalar.copy(
-                columns.rearrange("p (i t u) -> p i t u", i=len(tiles), u=2),
+                h_cols[tiles][:].bitcast(F32).rearrange("p (i t u) -> p i t u", i=len(tiles), u=2),
                 turned[:].rearrange("p (i u) t -> p i t u", u=2),
             )
 
-        def quantise_h(half, words):
-            h_w[half] = words
-            nc.vector.quantize_mx(out=words[:].bitcast(FP8X4), scales=h_s[half][:], in_=h_cols[half][:])
+        def quantise_h(tiles, on=None):
+            h_w[tiles] = held([P, P * len(tiles)], U32, "h_w%d" % tiles[0], on)
+            h_s[tiles] = held([P, P * len(tiles)], U8, "h_s%d" % tiles[0])
+            nc.vector.quantize_mx(out=h_w[tiles][:].bitcast(FP8X4), scales=h_s[tiles][:], in_=h_cols[tiles][:])
 
-        def out_matmul(half, n, b):
-            bank = bank_tile(b, [P, HALF])
-            nc.tensor.matmul_mx(
-                out=bank[:],
-                lhsT=wo_w[:, n * P : (n + 1) * P].bitcast(FP8X4),
-                lhsT_scale=wo_s[:, n * P : (n + 1) * P],
-                rhs=h_w[half][:].bitcast(FP8X4),
-                rhs_scale=h_s[half][:],
-                start=True,
-                stop=True,
-            )
+        def tokens(group):
+            first = GROUPS[group][0][0] * P
+            return first, sum(len(tiles) for tiles in GROUPS[group]) * P
+
+        def weights(group):
+            first, count = tokens(group)
+            return wgo_sb[:, first : first + count]
+
+        def out_matmul(group, n, b):
+            first, count = tokens(group)
+            bank = bank_tile(b, [P, count])
+            for tiles in GROUPS[group]:
+                j = tiles[0] * P - first
+                nc.tensor.matmul_mx(
+                    out=bank[:, j : j + P * len(tiles)],
+                    lhsT=wo_w[:, n * P : (n + 1) * P].bitcast(FP8X4),
+                    lhsT_scale=wo_s[:, n * P : (n + 1) * P],
+                    rhs=h_w[tiles][:].bitcast(FP8X4),
+                    rhs_scale=h_s[tiles][:],
+                    start=True,
+                    stop=True,
+                )
             return bank
 
-        def out_project(half, n, y, b):
-            nc.scalar.copy(y[:], out_matmul(half, n, b)[:])
+        def y_tile(group, n, on=None):
+            return held([P, tokens(group)[1]], F32, "y%d%d" % (group, n), on)
+
+        def y_copied(group, n, b, on=None):
+            y = y_tile(group, n, on)
+            nc.scalar.copy(y[:], out_matmul(group, n, b)[:])
             return y
 
-        def scatter(half, n, y):
-            nc.vector.tensor_tensor(
-                cache[n][:].indirect(entries(place, half * HALF, HALF)), y[:],
-                wgo_sb[:, half * HALF : (half + 1) * HALF], MULT,
-            )
+        def weighted_from_bank(group, n, bank):
+            y = y_tile(group, n)
+            nc.vector.tensor_tensor(y[:], bank[:], weights(group), MULT)
+            return y
+
+        def weighted_in_place(group, y):
+            nc.gpsimd.tensor_tensor(y[:], y[:], weights(group), MULT)
+            return y
+
+        def window(group, n):
+            return cache[n][:].indirect(entries(place, *tokens(group)))
+
+        def scatter_copy(group, n, y):
+            nc.vector.tensor_copy(window(group, n), y[:])
+
+        def scatter_weighted(group, n, y):
+            nc.vector.tensor_tensor(window(group, n), y[:], weights(group), MULT)
+
+        def right_copied(i):
+            right = held([P, H], F32, "right%d" % i)
+            nc.scalar.copy(in_order(right), from_bank(banks[RIGHT, i]))
+            return right
+
+        def times_right_copy(i, right):
+            h_rows[i] = held([P, H], BF16, "h_rows%d" % i)
+            nc.gpsimd.tensor_tensor(h_rows[i][:], right[:], gated[i][:], MULT)
 
         nc.gpsimd.memset(tab_s[:].bitcast(I32), 0)
 
         nc.sync.dma_start(pick[:], offs)
         nc.sync.dma_start(place[:], offs2)
         load_gate_scales(LEFT, (0,))
-        for q in range(4):
+        for m in range(4):
             nc.sync.dma_start(
-                out=tab_s[:].bitcast(I32)[32 * q : 32 * q + 8, :],
-                in_=tab_scales.bitcast(I32)[:, 4 * q : 4 * q + 4, :],
+                out=tab_s[:].bitcast(I32)[m:P:16, :],
+                in_=tab_scales.bitcast(I32)[:, m:16:4, :].rearrange("a q c -> q a c"),
             )
         load_table(0)
         load_gate_scales(LEFT, (1, 2, 3))
         load_gate_words(LEFT)
+        load_gate_scales(RIGHT, (0, 1))
         load_table(1)
-        load_gate_scales(RIGHT, range(4))
+        load_gate_scales(RIGHT, (2, 3))
 
         make_identity(nc, ident[:])
         for n in range(ROW_TILES):
             nc.gpsimd.memset(cache[n][:], 0.0)
 
         nc.vector.tensor_copy(v_s[0][:], tab_s[:].indirect(pick[:]))
-        nc.sync.dma_start(out=v_s[1][:].bitcast(I32)[0:100, :], in_=v_s[0][:].bitcast(I32)[4:104, :])
+        for q in range(4):
+            nc.sync.dma_start(
+                out=v_s[1][:].bitcast(I32)[32 * q : 32 * q + 4, :],
+                in_=v_s[0][:].bitcast(I32)[32 * q + 16 : 32 * q + 20, :],
+            )
         load_raw(LEFT, 0)
         load_raw(LEFT, 1)
 
@@ -289,42 +330,47 @@ def tile_list_gated_pair_terms_kernel(
         for i in range(3, 5):
             projection(RIGHT, i, i - 3)
         times_right_gate(nc.gpsimd, 4)
-        times_right_gate(nc.gpsimd, 5)
 
         times_right(0)
         times_right(1)
         turn((0, 1), 5)
         times_right(2)
-        turn((2,), 6)
         times_right(3)
-        turn((3,), 7)
-        projection(RIGHT, 5, 2)
-        late_gate(6, 5)
+        quantise_h((0, 1))
+        y_banks = [out_matmul(0, n, 2 + n) for n in range(2)]
+        times_right_gate(nc.gpsimd, 5, held([P, H], F32, "gated5_both", "h_cols0"))
+        late_gate(6, 0)
         times_right(4)
-        quantise_h(0, late_sig_bytes([P, HALF], U32, "h_w0", 5))
-        y_bank = out_matmul(0, 0, 0)
+        turn((2, 3), 6)
+        turn((4,), 7)
+        projection(RIGHT, 5, 5)
+        times_right_gate(nc.gpsimd, 6)
+        y02 = weighted_in_place(0, y_copied(0, 2, 4))
+        late_gate(7, 1)
+        y00, y01 = [weighted_from_bank(0, n, y_banks[n]) for n in range(2)]
+        scatter_copy(0, 0, y00)
         times_right(5)
-        late_gate(7, 6)
-        projection(RIGHT, 7, 1)
-        projection(RIGHT, 6, 2)
-        times_right_gate(nc.gpsimd, 6, held([P, H], F32, "gated6_both", "h_cols0"))
-        times_right_gate(nc.gpsimd, 7)
-        y_first = held([P, HALF], F32, "y00")
-        nc.vector.tensor_tensor(y_first[:], y_bank[:], wgo_sb[:, :HALF], MULT)
-        nc.vector.tensor_copy(cache[0][:].indirect(entries(place, 0, HALF)), y_first[:])
-        turn((4, 5), 3)
-        right7 = held([P, H], F32, "right7")
-        nc.scalar.copy(in_order(right7), from_bank(banks[RIGHT, 7]))
-        h_rows[7] = held([P, H], BF16, "h_rows7")
-        nc.gpsimd.tensor_tensor(h_rows[7][:], right7[:], gated[7][:], MULT)
-        times_right(6)
-        turn((6, 7), 4)
+        quantise_h((2, 3))
+        quantise_h((4,))
+        scatter_copy(0, 1, y01)
+        scatter_copy(0, 2, y02)
 
-        scatter(0, 1, out_project(0, 1, held([P, HALF], F32, "y01", "gated6"), 7))
-        quantise_h(1, held([P, HALF], U32, "h_w1"))
-        scatter(0, 2, out_project(0, 2, held([P, HALF], F32, "y02", "h_rows7"), 0))
+        y10, y11 = [y_copied(1, n, 2 + n) for n in range(2)]
+        projection(RIGHT, 6, 6)
+        projection(RIGHT, 7, 7)
+        right = {i: right_copied(i) for i in (6, 7)}
+        times_right_gate(nc.gpsimd, 7, held([P, H], F32, "gated7_both", "h_cols4"))
+        scatter_copy(1, 0, weighted_in_place(1, y10))
+        times_right_copy(6, right[6])
+        turn((5, 6), 0)
+        scatter_copy(1, 1, weighted_in_place(1, y11))
+        times_right_copy(7, right[7])
+        turn((7,), 1)
+        quantise_h((5, 6))
+        quantise_h((7,))
+        scatter_weighted(1, 2, y_copied(1, 2, 4, "h_rows7"))
         for n in range(ROW_TILES):
-            scatter(1, n, out_project(1, n, held([P, HALF], F32, "y1%d" % n), 3 + n))
+            scatter_weighted(2, n, y_copied(2, n, 5 + n))
 
         for n in range(ROW_TILES):
             nc.sync.dma_start(out=out[n * P : (n + 1) * P, :], in_=cache[n][:])

@@ -83,8 +83,9 @@ def tile_list_gated_pair_terms_kernel(
             rows = (wl, wr)[g][512 * a : 512 * (a + 1), :]
             nc.sync.dma_start(out=raw[g, a][:], in_=rows.rearrange("(p j) c -> p j c", j=4))
 
-        def load_table(a):
-            nc.sync.dma_start(out=tab_w[a][:], in_=tab_words[a].rearrange("p t i -> p (t i)").bitcast(I32))
+        def load_table(a, first=0, last=T):
+            words = tab_words[a].rearrange("p t i -> p (t i)").bitcast(I32)
+            nc.sync.dma_start(out=tab_w[a][:, first:last], in_=words[:, first:last])
 
         def load_gate_words(g):
             nc.sync.dma_start(
@@ -251,14 +252,14 @@ def tile_list_gated_pair_terms_kernel(
         nc.gpsimd.memset(tab_s[:].bitcast(I32), 0)
 
         nc.sync.dma_start(pick[:], offs)
-        nc.sync.dma_start(place[:], offs2)
+        load_table(0, 0, 512)
         load_gate_scales(LEFT, (0,))
         for m in range(4):
             nc.sync.dma_start(
                 out=tab_s[:].bitcast(I32)[m:P:16, :],
                 in_=tab_scales.bitcast(I32)[:, m:16:4, :].rearrange("a q c -> q a c"),
             )
-        load_table(0)
+        load_table(0, 512)
         load_gate_scales(LEFT, (1, 2, 3))
         load_gate_words(LEFT)
         load_gate_scales(RIGHT, (0, 1))
@@ -294,6 +295,7 @@ def tile_list_gated_pair_terms_kernel(
             )
         wgo_sb = placed([P, S], F32, "wgo_sb", AT_WGO)
         nc.sync.dma_start(out=wgo_sb[:], in_=wgo)
+        nc.sync.dma_start(place[:], offs2)
 
         for i in range(TILES):
             gate(LEFT, i, i, held([P, H], F32, "sig0%d" % i))

@@ -30,7 +30,6 @@ KIB = 1024
 AT_WL = (8 * KIB, 0)
 AT_TABLE_SCALES = 7 * KIB
 AT_TABLE = (16 * KIB, 34 * KIB)
-AT_RIGHT_GATE = 17 * KIB
 AT_WR = (19 * KIB, 27 * KIB)
 AT_WO_WORDS, AT_WO_SCALES, AT_WGO = 36 * KIB, 37 * KIB + 512, 38 * KIB
 AT_LATE_SIGS = 26 * KIB
@@ -70,7 +69,7 @@ def tile_list_gated_pair_terms_kernel(
         tab_s = placed([P, T], U8, "tab_s", AT_TABLE_SCALES)
         v_w = {}
         v_s = [held([P, S], U8, "v_s%d" % a) for a in range(PASSES)]
-        gate_w = {LEFT: held([P, PASSES * 2 * H], U8, "gate_w0")}
+        gate_w = [held([P, PASSES * 2 * H], U8, "gate_w%d" % g) for g in range(2)]
         gate_s = [held([P, PASSES * H], U8, "gate_s%d" % g) for g in range(2)]
         proj_s = [[held([P, H], U8, "proj_s%d%d" % (g, a)) for a in range(PASSES)] for g in range(2)]
         cache = [held([P, T2], F32, "cache%d" % n) for n in range(ROW_TILES)]
@@ -143,7 +142,7 @@ def tile_list_gated_pair_terms_kernel(
             return bank[:].rearrange("t (p u e) -> t u p e", u=2, e=2)
 
         def in_order(row):
-            return row[:].rearrange("t (u p e) -> t u p e", u=2, e=2)
+            return row[:, :].rearrange("t (u p e) -> t u p e", u=2, e=2)
 
         def gate(g, i, b, into):
             sig[g, i] = into
@@ -161,7 +160,7 @@ def tile_list_gated_pair_terms_kernel(
             banks[g, i] = project(b, i, lambda a: proj_w[g, a][:].bitcast(FP8X4), lambda a: proj_s[g][a][:])
 
         def times_left(i, into=None):
-            gated[i] = into or held([P, H], F32, "gated%d" % i)
+            gated[i] = held([P, H], F32, "gated%d" % i) if into is None else into
             nc.vector.tensor_tensor(in_order(gated[i]), from_bank(banks[LEFT, i]), in_order(sig[LEFT, i]), MULT)
 
         def times_right_gate(engine, i, into=None):
@@ -277,11 +276,10 @@ def tile_list_gated_pair_terms_kernel(
                 in_=v_s[0][:].bitcast(I32)[32 * q + 16 : 32 * q + 20, :],
             )
         load_raw(LEFT, 0)
+        load_gate_words(RIGHT)
         load_raw(LEFT, 1)
 
         gather_words(0)
-        gate_w[RIGHT] = placed([P, PASSES * 2 * H], U8, "gate_w1", AT_RIGHT_GATE)
-        load_gate_words(RIGHT)
         load_raw(RIGHT, 0)
         gather_words(1)
         load_raw(RIGHT, 1)
@@ -297,33 +295,32 @@ def tile_list_gated_pair_terms_kernel(
         nc.sync.dma_start(out=wgo_sb[:], in_=wgo)
         nc.sync.dma_start(place[:], offs2)
 
-        for i in range(TILES):
-            gate(LEFT, i, i, held([P, H], F32, "sig0%d" % i))
+        for i, b in enumerate((0, 4, 6, 1, 2, 3, 0, 4)):
+            gate(LEFT, i, b, held([P, H], F32, "sig0%d" % i))
+        gate(RIGHT, 2, 7, held([P, H], F32, "sig12"))
+        first_sigs = held([P, 2 * H], F32, "first_sigs")
+        for i in range(2):
+            gate(RIGHT, i, 5 + i, first_sigs[:, H * i : H * (i + 1)])
         for a in range(PASSES):
             weave(nc.vector.tensor_copy, LEFT, a)
             quantise_weight(LEFT, a)
 
-        for i in range(2):
-            projection(LEFT, i, 3 + i)
-        for b, i in enumerate((2, 0, 1)):
-            gate(RIGHT, i, b, held([P, H], F32, "sig1%d" % i))
-        for i in range(2, 5):
-            projection(LEFT, i, i - 2)
+        for i, b in enumerate((1, 2, 3, 0)):
+            projection(LEFT, i, b)
         weave(nc.scalar.copy, RIGHT, 0)
         weave(nc.scalar.copy, RIGHT, 1, placed([P, H, 4], BF16, "woven11", AT_LAST_WOVEN))
         both_gates = held([P, H], F32, "both_gates", "woven01")
         nc.gpsimd.tensor_tensor(both_gates[:], sig[LEFT, 2][:], sig[RIGHT, 2][:], MULT)
         sig[LEFT, 2] = both_gates
-        for i in range(3):
+        first_gated = held([P, 2 * H], F32, "first_gated")
+        for i in range(4):
+            times_left(i, first_gated[:, H * i : H * (i + 1)] if i < 2 else None)
+            projection(LEFT, 4 + i, (1 + i) % 4)
+        nc.gpsimd.tensor_tensor(first_gated[:], first_gated[:], first_sigs[:], MULT)
+        for i in range(4, 7):
             times_left(i)
-            projection(LEFT, 5 + i, (3 + i) % 5)
-            if i < 2:
-                times_right_gate(nc.gpsimd, i)
-        for i in range(3, 6):
-            times_left(i)
-            late_gate(i, i - 2)
-        times_left(6)
-        quantise_weight(RIGHT, 0, "sig11")
+            late_gate(i - 1, i - 3)
+        quantise_weight(RIGHT, 0, "first_sigs")
         quantise_weight(RIGHT, 1)
         for i in range(3):
             projection(RIGHT, i, 5 + i)

@@ -36,6 +36,8 @@ AT_LATE_SIGS = 26 * KIB
 AT_LAST_WOVEN = 42 * KIB
 GROUPS = (((0, 1),), ((2, 3), (4,)), ((5, 6), (7,)))
 EARLY_SIGS = 3
+WHOLE = (slice(0, H),)
+HALVES = (slice(0, H // 2), slice(H // 2, H))
 PIECES = ((0, 256), (256, 256), (512, 512))
 
 
@@ -109,20 +111,22 @@ def tile_list_gated_pair_terms_kernel(
                 for j in range(0, count, P):
                     v_w[a, (first + j) // P] = piece[:, j : j + P]
 
-        def weave(copy, g, a, into=None):
+        def weave(copy, g, a, parts, into=None):
             woven[g, a] = into or held([P, H, 4], BF16, "woven%d%d" % (g, a))
-            copy(
-                woven[g, a][:].rearrange("p (c i) j -> p c j i", i=4),
-                raw[g, a][:].rearrange("p j (c i) -> p c j i", i=4),
-            )
+            for columns in parts:
+                copy(
+                    woven[g, a][:, columns, :].rearrange("p (c i) j -> p c j i", i=4),
+                    raw[g, a][:, :, columns].rearrange("p j (c i) -> p c j i", i=4),
+                )
 
-        def quantise_weight(g, a, on=None):
+        def quantise_weight(g, a, parts, on=None):
             proj_w[g, a] = held([P, H], U32, "proj_w%d%d" % (g, a), on)
-            nc.vector.quantize_mx(
-                out=proj_w[g, a][:].bitcast(FP8X4),
-                scales=proj_s[g][a][:],
-                in_=woven[g, a][:].rearrange("p c j -> p (c j)"),
-            )
+            for columns in parts:
+                nc.vector.quantize_mx(
+                    out=proj_w[g, a][:, columns].bitcast(FP8X4),
+                    scales=proj_s[g][a][:, columns],
+                    in_=woven[g, a][:, columns, :].rearrange("p c j -> p (c j)"),
+                )
 
         def project(b, i, words, scales):
             bank = bank_tile(b, [P, H])
@@ -302,13 +306,13 @@ def tile_list_gated_pair_terms_kernel(
         for i in range(2):
             gate(RIGHT, i, 5 + i, first_sigs[:, H * i : H * (i + 1)])
         for a in range(PASSES):
-            weave(nc.vector.tensor_copy, LEFT, a)
-            quantise_weight(LEFT, a)
+            weave(nc.vector.tensor_copy, LEFT, a, HALVES)
+            quantise_weight(LEFT, a, HALVES)
 
         for i, b in enumerate((1, 2, 3, 0)):
             projection(LEFT, i, b)
-        weave(nc.scalar.copy, RIGHT, 0)
-        weave(nc.scalar.copy, RIGHT, 1, placed([P, H, 4], BF16, "woven11", AT_LAST_WOVEN))
+        weave(nc.scalar.copy, RIGHT, 0, WHOLE)
+        weave(nc.scalar.copy, RIGHT, 1, HALVES, placed([P, H, 4], BF16, "woven11", AT_LAST_WOVEN))
         both_gates = held([P, H], F32, "both_gates", "woven01")
         nc.gpsimd.tensor_tensor(both_gates[:], sig[LEFT, 2][:], sig[RIGHT, 2][:], MULT)
         sig[LEFT, 2] = both_gates
@@ -320,8 +324,8 @@ def tile_list_gated_pair_terms_kernel(
         for i in range(4, 7):
             times_left(i)
             late_gate(i - 1, i - 3)
-        quantise_weight(RIGHT, 0, "first_sigs")
-        quantise_weight(RIGHT, 1)
+        quantise_weight(RIGHT, 0, WHOLE, "first_sigs")
+        quantise_weight(RIGHT, 1, HALVES)
         for i in range(3):
             projection(RIGHT, i, 5 + i)
         times_left(7, placed([P, H], F32, "gated7", AT_LAST_WOVEN + 2 * KIB))

from contextlib import ExitStack

import concourse.mybir as mybir
from concourse.masks import make_identity

K, T, S, H, N, T2 = 1024, 2048, 1024, 512, 384, 2048
FLOPS = 2 * (4 * K * H * S + H * N * S)

F32 = mybir.dt.float32
BF16 = mybir.dt.bfloat16
I32 = mybir.dt.int32
U32 = mybir.dt.uint32
U16 = mybir.dt.uint16
U8 = mybir.dt.uint8
FP8X4 = mybir.dt.float8_e4m3fn_x4
FP4X4 = mybir.dt.float4_e2m1fn_x4
MULT = mybir.AluOpType.mult
SIGMOID = mybir.ActivationFunctionType.Sigmoid

P = 128
PASSES = K // 512
HALF = S // 2
CHUNK = 256
ROW_TILES = N // P
LEFT, RIGHT = 0, 1

TILES = S // P
KIB = 1024

AT_WL = (8 * KIB, 0)
AT_TABLE_SCALES = 7 * KIB
AT_TABLE = (16 * KIB, 34 * KIB)
AT_WR = (19 * KIB, 27 * KIB)
AT_WO_WORDS, AT_WO_SCALES, AT_WGO = 36 * KIB, 37 * KIB + 512, 38 * KIB
AT_LATE_SIGS = 26 * KIB
AT_LAST_WOVEN = 42 * KIB
GROUPS = (((0, 1),), ((2, 3), (4,)), ((5, 6), (7,)))
EARLY_SIGS = 3
WHOLE = (slice(0, H),)
HALVES = (slice(0, H // 2), slice(H // 2, H))
PIECES = ((0, 256), (256, 256), (512, 512))


def tile_list_gated_pair_terms_kernel(
    tc, tab_words, tab_scales, offs, wl, wr, gl_words, gl_scales, gr_words, gr_scales,
    wo_words, wo_scales, wgo, offs2, out,
):
    nc = tc.nc
    with ExitStack() as ctx:
        lists = ctx.enter_context(tc.tile_pool(name="lists", bufs=1))
        keep = ctx.enter_context(tc.tile_pool(name="keep", bufs=1))
        by_hand = ctx.enter_context(tc.tile_pool(name="by_hand", bufs=1))
        psum = ctx.enter_context(tc.psum_pool(name="psum", bufs=1))

        def held(shape, dtype, name, on=None):
            return keep.tile(shape, dtype, name=name, tag=on or name, align_bytes=64)

        def placed(shape, dtype, name, offset):
            return by_hand.tile(shape, dtype, name=name, align_bytes=64, offset=offset)

        def bank_tile(b, shape):
            return psum.tile(shape, F32, name="bank", tag="bank%d" % b)

        def late_sig_bytes(shape, dtype, name, i):
            return placed(shape, dtype, name, AT_LATE_SIGS + 2 * KIB * (i - EARLY_SIGS))

        pick = lists.tile([P, S // 16], U16, name="pick")
        place = lists.tile([P, S // 16], U16, name="place")

        tab_w = [placed([P, T], I32, "tab_w%d" % a, AT_TABLE[a]) for a in range(PASSES)]
        tab_s = placed([P, T], U8, "tab_s", AT_TABLE_SCALES)
        v_w = {}
        v_s = [held([P, S], U8, "v_s%d" % a) for a in range(PASSES)]
        gate_w = [held([P, PASSES * 2 * H], U8, "gate_w%d" % g) for g in range(2)]
        gate_s = [held([P, PASSES * H], U8, "gate_s%d" % g) for g in range(2)]
        proj_s = [[held([P, H], U8, "proj_s%d%d" % (g, a)) for a in range(PASSES)] for g in range(2)]
        cache = [held([P, T2], F32, "cache%d" % n) for n in range(ROW_TILES)]
        ident = held([P, P], F32, "ident")
        raw, woven, proj_w, banks, sig, gated, h_rows = {}, {}, {}, {}, {}, {}, {}
        h_cols, h_w, h_s = {}, {}, {}

        def load_raw(g, a):
            raw[g, a] = placed([P, 4, H], F32, "raw%d%d" % (g, a), (AT_WL, AT_WR)[g][a])
            rows = (wl, wr)[g][512 * a : 512 * (a + 1), :]
            nc.sync.dma_start(out=raw[g, a][:], in_=rows.rearrange("(p j) c -> p j c", j=4))

        def load_table(a, first=0, last=T):
            words = tab_words[a].rearrange("p t i -> p (t i)").bitcast(I32)
            nc.sync.dma_start(out=tab_w[a][:, first:last], in_=words[:, first:last])

        def load_gate_words(g):
            nc.sync.dma_start(
                out=gate_w[g][:].bitcast(I32).rearrange("p (a c) -> p a c", a=PASSES),
                in_=(gl_words, gr_words)[g].bitcast(I32).rearrange("a p c -> p a c"),
            )

        def load_gate_scales(g, quadrants):
            for q in quadrants:
                nc.sync.dma_start(
                    out=gate_s[g][:].bitcast(I32)[32 * q : 32 * q + 4, :],
                    in_=(gl_scales, gr_scales)[g].bitcast(I32)[:, 4 * q : 4 * q + 4, :].rearrange("a m c -> m a c"),
                )

        def entries(offsets, first, count):
            return offsets[:, first // 16 : (first + count) // 16]

        def gather_words(a):
            for first, count in PIECES:
                piece = held([P, count], U32, "v_w%d_%d" % (a, first))
                nc.vector.tensor_copy(piece[:], tab_w[a][:].bitcast(U32).indirect(entries(pick, first, count)))
                for j in range(0, count, P):
                    v_w[a, (first + j) // P] = piece[:, j : j + P]

        def weave(copy, g, a, parts, into=None):
            woven[g, a] = into or held([P, H, 4], BF16, "woven%d%d" % (g, a))
            for columns in parts:
                copy(
                    woven[g, a][:, columns, :].rearrange("p (c i) j -> p c j i", i=4),
                    raw[g, a][:, :, columns].rearrange("p j (c i) -> p c j i", i=4),
                )

        def quantise_weight(g, a, parts, on=None):
            proj_w[g, a] = held([P, H], U32, "proj_w%d%d" % (g, a), on)
            for columns in parts:
                nc.vector.quantize_mx(
                    out=proj_w[g, a][:, columns].bitcast(FP8X4),
                    scales=proj_s[g][a][:, columns],
                    in_=woven[g, a][:, columns, :].rearrange("p c j -> p (c j)"),
                )

        def project(b, i, words, scales):
            bank = bank_tile(b, [P, H])
            for a in range(PASSES):
                nc.tensor.matmul_mx(
                    out=bank[:],
                    lhsT=v_w[a, i].bitcast(FP8X4),
                    lhsT_scale=v_s[a][:, i * P : (i + 1) * P],
                    rhs=words(a),
                    rhs_scale=scales(a),
                    start=(a == 0),
                    stop=(a == PASSES - 1),
                )
            return bank

        def from_bank(bank):
            return bank[:].rearrange("t (p u e) -> t u p e", u=2, e=2)

        def in_order(row):
            return row[:, :].rearrange("t (u p e) -> t u p e", u=2, e=2)

        def gate(g, i, b, into):
            sig[g, i] = into
            bank = project(
                b, i,
                lambda a: gate_w[g][:, 2 * H * a : 2 * H * (a + 1)].bitcast(FP4X4),
                lambda a: gate_s[g][:, H * a : H * (a + 1)],
            )
            nc.scalar.activation(in_order(into), from_bank(bank), SIGMOID)

        def late_gate(i, b):
            gate(RIGHT, i, b, late_sig_bytes([P, H], F32, "sig1%d" % i, i))

        def projection(g, i, b):
            banks[g, i] = project(b, i, lambda a: proj_w[g, a][:].bitcast(FP8X4), lambda a: proj_s[g][a][:])

        def times_left(i, into=None):
            gated[i] = held([P, H], F32, "gated%d" % i) if into is None else into
            nc.vector.tensor_tensor(in_order(gated[i]), from_bank(banks[LEFT, i]), in_order(sig[LEFT, i]), MULT)

        def times_right_gate(engine, i, into=None):
            source = gated[i]
            gated[i] = into or source
            engine.tensor_tensor(gated[i][:], source[:], sig[RIGHT, i][:], MULT)

        def times_right(i, into=None):
            h_rows[i] = into or held([P, H], BF16, "h_rows%d" % i)
            nc.vector.tensor_tensor(in_order(h_rows[i]), from_bank(banks[RIGHT, i]), in_order(gated[i]), MULT)

        def turn(tiles, b):
            turned = bank_tile(b, [P, 2 * len(tiles), P])
            for sub, i in enumerate(tiles):
                for u in range(2):
                    words = h_rows[i][:].bitcast(F32)[:, P * u : P * (u + 1)]
                    nc.tensor.transpose(turned[:, 2 * sub + u, :], words, ident[:])
            h_cols[tiles] = held([P, 4 * P * len(tiles)], BF16, "h_cols%d" % tiles[0])
            nc.scalar.copy(
                h_cols[tiles][:].bitcast(F32).rearrange("p (i t u) -> p i t u", i=len(tiles), u=2),
                turned[:].rearrange("p (i u) t -> p i t u", u=2),
            )

        def quantise_h(tiles, on=None):
            h_w[tiles] = held([P, P * len(tiles)], U32, "h_w%d" % tiles[0], on)
            h_s[tiles] = held([P, P * len(tiles)], U8, "h_s%d" % tiles[0])
            nc.vector.quantize_mx(out=h_w[tiles][:].bitcast(FP8X4), scales=h_s[tiles][:], in_=h_cols[tiles][:])

        def tokens(group):
            first = GROUPS[group][0][0] * P
            return first, sum(len(tiles) for tiles in GROUPS[group]) * P

        def weights(group):
            first, count = tokens(group)
            return wgo_sb[:, first : first + count]

        def out_matmul(group, n, b):
            first, count = tokens(group)
            bank = bank_tile(b, [P, count])
            for tiles in GROUPS[group]:
                j = tiles[0] * P - first
                nc.tensor.matmul_mx(
                    out=bank[:, j : j + P * len(tiles)],
                    lhsT=wo_w[:, n * P : (n + 1) * P].bitcast(FP8X4),
                    lhsT_scale=wo_s[:, n * P : (n + 1) * P],
                    rhs=h_w[tiles][:].bitcast(FP8X4),
                    rhs_scale=h_s[tiles][:],
                    start=True,
                    stop=True,
                )
            return bank

        def y_tile(group, n, on=None):
            return held([P, tokens(group)[1]], F32, "y%d%d" % (group, n), on)

        def y_copied(group, n, b, on=None):
            y = y_tile(group, n, on)
            nc.scalar.copy(y[:], out_matmul(group, n, b)[:])
            return y

        def weighted_from_bank(group, n, bank):
            y = y_tile(group, n)
            nc.vector.tensor_tensor(y[:], bank[:], weights(group), MULT)
            return y

        def weighted_in_place(group, y):
            nc.gpsimd.tensor_tensor(y[:], y[:], weights(group), MULT)
            return y

        def window(group, n):
            return cache[n][:].indirect(entries(place, *tokens(group)))

        def scatter_copy(group, n, y):
            nc.vector.tensor_copy(window(group, n), y[:])

        def scatter_weighted(group, n, y):
            nc.vector.tensor_tensor(window(group, n), y[:], weights(group), MULT)

        def right_copied(i):
            right = held([P, H], F32, "right%d" % i)
            nc.scalar.copy(in_order(right), from_bank(banks[RIGHT, i]))
            return right

        def times_right_copy(i, right):
            h_rows[i] = held([P, H], BF16, "h_rows%d" % i)
            nc.gpsimd.tensor_tensor(h_rows[i][:], right[:], gated[i][:], MULT)

        nc.gpsimd.memset(tab_s[:].bitcast(I32), 0)

        nc.sync.dma_start(pick[:], offs)
        load_table(0, 0, 512)
        load_gate_scales(LEFT, (0,))
        for m in range(4):
            nc.sync.dma_start(
                out=tab_s[:].bitcast(I32)[m:P:16, :],
                in_=tab_scales.bitcast(I32)[:, m:16:4, :].rearrange("a q c -> q a c"),
            )
        load_table(0, 512)
        load_gate_scales(LEFT, (1, 2, 3))
        load_gate_words(LEFT)
        load_gate_scales(RIGHT, (0, 1))
        load_table(1)
        load_gate_scales(RIGHT, (2, 3))

        make_identity(nc, ident[:])
        for n in range(ROW_TILES):
            nc.gpsimd.memset(cache[n][:], 0.0)

        nc.vector.tensor_copy(v_s[0][:], tab_s[:].indirect(pick[:]))
        for q in range(4):
            nc.sync.dma_start(
                out=v_s[1][:].bitcast(I32)[32 * q : 32 * q + 4, :],
                in_=v_s[0][:].bitcast(I32)[32 * q + 16 : 32 * q + 20, :],
            )
        load_raw(LEFT, 0)
        load_gate_words(RIGHT)
        load_raw(LEFT, 1)

        gather_words(0)
        load_raw(RIGHT, 0)
        gather_words(1)
        load_raw(RIGHT, 1)
        wo_w = placed([P, N], I32, "wo_w", AT_WO_WORDS)
        nc.sync.dma_start(out=wo_w[:], in_=wo_words[0].rearrange("p c i -> p (c i)").bitcast(I32))
        wo_s = placed([P, N], U8, "wo_s", AT_WO_SCALES)
        for q in range(4):
            nc.sync.dma_start(
                out=wo_s[:].bitcast(I32)[32 * q : 32 * q + 4, :],
                in_=wo_scales[0].bitcast(I32)[4 * q : 4 * q + 4, :],
            )
        wgo_sb = placed([P, S], F32, "wgo_sb", AT_WGO)
        nc.sync.dma_start(out=wgo_sb[:], in_=wgo)
        nc.sync.dma_start(place[:], offs2)

        for i, b in enumerate((0, 4, 6, 1, 2, 3, 0, 4)):
            gate(LEFT, i, b, held([P, H], F32, "sig0%d" % i))
        gate(RIGHT, 2, 7, held([P, H], F32, "sig12"))
        first_sigs = held([P, 2 * H], F32, "first_sigs")
        for i in range(2):
            gate(RIGHT, i, 5 + i, first_sigs[:, H * i : H * (i + 1)])
        for a in range(PASSES):
            weave(nc.vector.tensor_copy, LEFT, a, HALVES)
            quantise_weight(LEFT, a, HALVES)

        for i, b in enumerate((1, 2, 3, 0)):
            projection(LEFT, i, b)
        weave(nc.scalar.copy, RIGHT, 0, WHOLE)
        weave(nc.scalar.copy, RIGHT, 1, HALVES, placed([P, H, 4], BF16, "woven11", AT_LAST_WOVEN))
        both_gates = held([P, H], F32, "both_gates", "woven01")
        nc.gpsimd.tensor_tensor(both_gates[:], sig[LEFT, 2][:], sig[RIGHT, 2][:], MULT)
        sig[LEFT, 2] = both_gates
        first_gated = held([P, 2 * H], F32, "first_gated")
        for i in range(4):
            times_left(i, first_gated[:, H * i : H * (i + 1)] if i < 2 else None)
            projection(LEFT, 4 + i, (1 + i) % 4)
        nc.gpsimd.tensor_tensor(first_gated[:], first_gated[:], first_sigs[:], MULT)
        for i in range(4, 7):
            times_left(i)
            late_gate(i - 1, i - 3)
        quantise_weight(RIGHT, 0, WHOLE, "first_sigs")
        quantise_weight(RIGHT, 1, HALVES)
        for i in range(3):
            projection(RIGHT, i, 5 + i)
        times_left(7, placed([P, H], F32, "gated7", AT_LAST_WOVEN + 2 * KIB))
        times_right_gate(nc.gpsimd, 3, placed([P, H], F32, "gated3_both", AT_LAST_WOVEN))
        for i in range(3, 5):
            projection(RIGHT, i, i - 3)
        times_right_gate(nc.gpsimd, 4)

        times_right(0)
        times_right(1)
        turn((0, 1), 5)
        times_right(2)
        times_right(3)
        quantise_h((0, 1))
        y_banks = [out_matmul(0, n, 2 + n) for n in range(2)]
        times_right_gate(nc.gpsimd, 5, held([P, H], F32, "gated5_both", "h_cols0"))
        late_gate(6, 0)
        times_right(4)
        turn((2, 3), 6)
        turn((4,), 7)
        projection(RIGHT, 5, 5)
        times_right_gate(nc.gpsimd, 6)
        y02 = weighted_in_place(0, y_copied(0, 2, 4))
        late_gate(7, 1)
        y00, y01 = [weighted_from_bank(0, n, y_banks[n]) for n in range(2)]
        scatter_copy(0, 0, y00)
        times_right(5)
        quantise_h((2, 3))
        quantise_h((4,))
        scatter_copy(0, 1, y01)
        scatter_copy(0, 2, y02)

        y10, y11 = [y_copied(1, n, 2 + n) for n in range(2)]
        projection(RIGHT, 6, 6)
        projection(RIGHT, 7, 7)
        right = {i: right_copied(i) for i in (6, 7)}
        times_right_gate(nc.gpsimd, 7, held([P, H], F32, "gated7_both", "h_cols4"))
        scatter_copy(1, 0, weighted_in_place(1, y10))
        times_right_copy(6, right[6])
        turn((5, 6), 0)
        scatter_copy(1, 1, weighted_in_place(1, y11))
        times_right_copy(7, right[7])
        turn((7,), 1)
        quantise_h((5, 6))
        quantise_h((7,))
        scatter_weighted(1, 2, y_copied(1, 2, 4, "h_rows7"))
        for n in range(ROW_TILES):
            scatter_weighted(2, n, y_copied(2, n, 5 + n))

        for n in range(ROW_TILES):
            nc.sync.dma_start(out=out[n * P : (n + 1) * P, :], in_=cache[n][:])
